import numpy as np, ml_dtypes
CORES = [16,18,20,22]
N = 4
import mx_ref
BF = ml_dtypes.bfloat16
def gentries(a):
    return np.ascontiguousarray(a.reshape(8, 16, -1).transpose(0, 2, 1)).reshape(8, -1)
def gtable(e):
    e = np.asarray(e); return np.ascontiguousarray(e.reshape(8, -1, 16).transpose(0, 2, 1)).reshape(128, -1).astype(np.int32)
def gcols(t, e):
    v = np.concatenate([t.reshape(8, 16, -1, 4), np.zeros((8, 16, 1, 4), BF)], axis=2)
    return np.ascontiguousarray(np.stack([v[g][:, e[g]] for g in range(8)])).reshape(128, -1)
def tile(rs):
    return np.stack(rs, axis=2).reshape(128, -1).astype(BF)
def pick(q, e):
    c = np.concatenate([q[0].reshape(128, -1, 4), np.zeros((128, 1, 4), np.uint8)], axis=1); s = np.concatenate([q[1], np.ones((16, 1), np.uint8)], axis=1)
    return (np.ascontiguousarray(c[:, e].reshape(128, -1)), np.ascontiguousarray(s[:, e]))
def join(*qs):
    return (np.concatenate([q[0] for q in qs], axis=1), np.concatenate([q[1] for q in qs], axis=1))
def put(q, e, v):
    c, s = q[0].reshape(128, -1, 4).copy(), q[1].copy(); c[:, e] = v[0].reshape(128, -1, 4); s[:, e] = v[1]
    return (c.reshape(128, -1), s)
def pk(c, s):
    return (np.ascontiguousarray(c), mx_ref.live(s))
def emit(q):
    return q[0], q[1]
def packed(v, rng):
    q = [mx_ref.quantize(np.ascontiguousarray(v[r])) for r in range(N)]
    return np.stack([a for a, b in q]), np.stack([mx_ref.plane(b, rng) for a, b in q])
def values_of_codes():
    e, c = np.zeros((128, 128, 4), np.float32), np.zeros((128, 2, 4), np.uint8)
    e[np.arange(128), np.arange(128), 0] = 1
    c[:127, :, 0] = np.arange(256).reshape(2, 128).T[:127]
    return mx_ref.matmul(mx_ref.quantize(e.reshape(128, 512).astype(BF)), (c.reshape(128, 8), np.full((16, 2), 127, np.uint8))).T.reshape(-1).astype(np.float64)
CODE_VALUE, SCALE_VALUE = values_of_codes(), 2.0 ** (np.arange(256) - 127.0)
def decode(q):
    return (CODE_VALUE[q[0]].reshape(16, 8, -1, 4) * SCALE_VALUE[q[1]][:, None, :, None] + 0.0).reshape(128, -1).astype(np.float32)
def f(rng, *shape):
    return mx_ref.flush((rng.standard_normal(shape, dtype=np.float32) * np.exp2(rng.integers(-2, 3, shape[:-1] + (1,)))).astype(BF))
def wide(rng, *shape, cols=0):
    v = rng.standard_normal(shape, dtype=np.float32) * np.exp2(rng.integers(-12, 13, shape)).astype(np.float32)
    if cols: v *= np.repeat(np.exp2(rng.integers(-cols, cols + 1, shape[:-2] + (1, shape[-1] // 4))) * (rng.random(shape[:-2] + (1, shape[-1] // 4)) > 0.0625), 4, axis=-1).astype(np.float32)
    return mx_ref.flush(v.astype(BF))
C, K, A, B, R = 192, 64, 8, 2, 3
STEP = [1, 2, 3]
def classes(key):
    c, one, two = np.zeros((8, C), int), np.full((8, K), -1), np.full((8, K), -1)
    for g in range(8):
        first, mine = np.unique(key[g], return_index=True, return_inverse=True)[1:]
        low = np.sort(first)
        c[g] = np.searchsorted(low, first[mine])
        for k in range(len(low)):
            m = np.flatnonzero(c[g] == k)
            one[g, k] = m[0]
            two[g, k] = m[min(1, len(m) - 1)]
    return c, one, two
def numbers_of(rng):
    return {"x": np.array(f(rng, N, 128, 4 * C)), "u": np.array(f(rng, N, 128, 512)), "v": np.array(f(rng, N, 128, 512))}
def lists_of(rng):
    return {"nx": rng.integers(0, C, (N, 8, C)), "co": rng.integers(0, K, (N, 8, C))}
def stored(l):
    return {k: np.stack([gtable(e) for e in l[k]]) for k in ("nx", "co")}
def weights(rng, w):
    c, p = packed(w, rng)
    return {"wc": c, "ws": p}
def quiet(rng):
    w = np.array(f(rng, N, 128, 2048)).reshape(N, 8, 16, 4, 8, 16, 4)
    w[:, :, :8] = 0
    w[:, :, :, :, :, :8] = 0
    return weights(rng, w.reshape(N, 128, 2048))
def marked(d, m, k):
    x = d["x"].reshape(N, 8, 16, C, 4)
    u = d["u"].reshape(N, 128, 128, 4)
    x[:, :, :8] = 0
    k = k.astype(np.float32)
    for i in range(2):
        x[:, :, i, :, :2] = m[:, :, :, i].astype(np.float32).astype(BF)
        u[:, :, i::16] = 0
        for h in range(i, 128, 16):
            u[:, h, h, 0] = k.astype(BF)
            u[:, h, h, 1] = (-k).astype(BF)
    return {"x": x.reshape(N, 128, 4 * C), "u": u.reshape(N, 128, 512), "v": d["v"]}
def setup_inputs(rng):
    return {**numbers_of(rng), **stored(lists_of(rng)), **weights(rng, f(rng, N, 128, 2048))}
def setup_inputs_full(rng):
    d, l = numbers_of(rng), lists_of(rng)
    o = rng.permutation(N)
    bits = np.zeros((N, 8, C), int)
    for r in range(N):
        e = np.argsort(rng.random((8, C)), axis=1)
        if o[r] % 4 == 3:
            l["co"][r] = rng.integers(0, K, (8, 1))
            bits[r] = e % (1 + rng.permutation(8) % 4)[:, None]
        else:
            k, one, two = classes(np.minimum(e, K - 1) if o[r] % 4 == 1 else e % K)
            l["co"][r] = k % A + A * rng.integers(0, K // A, (8, C))
            l["nx"][r] = np.take_along_axis(one, k // A % B + B * rng.integers(0, K // B, (8, C)), axis=1)
            bits[r] = k // (A * B)
    m = np.zeros((N, 8, C, 2, 2))
    m[:, :, :, 0] = 2 * (np.arange(2) == (bits >> 1)[:, :, :, None])
    m[:, :, :, 1] = 2 * (np.arange(2) == (bits & 1)[:, :, :, None])
    return {**marked(d, m, np.ones(N)), **stored(l), **quiet(rng)}
def setup_inputs_near(rng):
    d, l = numbers_of(rng), lists_of(rng)
    p = np.array([[0, 0], [2, 2], [3, 2], [2, 3], [2, 0], [0, 2]])
    e = np.argsort(rng.random((N, 8, C)), axis=2)
    h = np.argsort(rng.random((N, 8, C)), axis=2)
    m = np.stack([p[e // 4 % 6], p[h % 6]], axis=3) * 2.0 ** np.array([-30, -12, 0, 28])[e % 4][:, :, :, None, None]
    k = np.where(rng.permutation(N) < N // 2, 2.0 ** -30, 1.0)
    return {**marked(d, m, k), **stored(l), **quiet(rng)}
def setup_inputs_lists(rng):
    d, l = numbers_of(rng), lists_of(rng)
    o = rng.permutation(N)
    x = d["x"].reshape(N, 128, C, 4)
    for r in range(N):
        a = x[r][:, :2].copy()
        if o[r] % 4 == 0: l["nx"][r] = np.arange(C)
        if o[r] % 4 == 1: l["nx"][r] = rng.integers(0, C, (8, 1))
        if o[r] % 4 == 2:
            l["nx"][r] = C - 1 - np.arange(C)
            a[:, 1] = 0
            x[r] = a[:, rng.permutation(C) % 2]
        if o[r] % 4 == 3:
            l["co"][r] = rng.integers(0, K, (8, 1))
            x[r] = a[:, np.zeros(C, int)]
    return {"x": x.reshape(N, 128, 4 * C), "u": d["u"], "v": d["v"], **stored(l), **weights(rng, f(rng, N, 128, 2048))}
def setup_inputs_huge(rng):
    d, l = numbers_of(rng), lists_of(rng)
    o = rng.permutation(N)
    c = np.stack([rng.permutation(C) % 2 * 2.0 - 1.0 for r in range(N)])
    c[o == 0] = 1
    c[o == 1] = -1
    p = rng.random((N, 128, C, 4))
    x = np.where(c[:, None, :, None] < 0, -2.0 ** 30 * (1 - 0.125 * p), 2.0 ** 28 * (1 - 0.5 * p))
    k = np.stack([rng.permutation(8) % 4 for r in range(N)])
    s = 1.0 - 2.0 * np.stack([k >> 1, k & 1], axis=2)
    u = d["u"].reshape(N, 128, 8, 16, 4)
    a = 2.0 ** 30 * (1 - 0.25 * rng.random((N, 128, 8, 2, 4))) * s[:, None, :, :, None]
    u[:, :, :, :2] = a.astype(np.float32).astype(BF)
    w = np.zeros((N, 128, 4, 128, 4), np.float32)
    i = np.arange(128)
    for b in range(4): w[:, i, b, i, b] = 8
    return {"x": x.astype(np.float32).reshape(N, 128, 4 * C).astype(BF), "u": u.reshape(N, 128, 512), "v": d["v"], **stored(l), **weights(rng, w.reshape(N, 128, 2048).astype(BF))}
def setup_inputs_spread(rng):
    d = setup_inputs(rng)
    d["x"] = wide(rng, N, 128, 4 * C, cols=6)
    return d
def check_inputs(d):
    b = []
    for k in ("x", "u", "v"):
        a = np.abs(d[k].astype(np.float32))
        if not (np.isfinite(a).all() and ((a == 0) | (a >= 2.0 ** -30) & (a <= 2.0 ** 30)).all()): b.append("a value of " + k)
    if ((d["nx"] < 0) | (d["nx"] >= C)).any(): b.append("an entry of nx")
    if ((d["co"] < 0) | (d["co"] >= K)).any(): b.append("an entry of co")
    if ((d["wc"] == 0x7F) | (d["wc"] == 0xFF)).any(): b.append("a code of wc is no number")
    for r in range(N):
        s = mx_ref.live(d["ws"][r])
        if ((s > 1) & (s < 64) | (s > 191)).any(): b.append("a scale of ws")
    return b
def reference(x, u, v, nx, co, wc, ws):
    qu = [mx_ref.quantize(u[r]) for r in range(N)]
    lay = [pk(wc[r], ws[r]) for r in range(N)]
    now = [x[r] for r in range(N)]
    to = [gentries(nx[r]).astype(np.int64) for r in range(N)]
    cl = [gentries(co[r]).astype(np.int64) for r in range(N)]
    for t in range(R):
        held, sent = [], []
        for r in range(N):
            q = mx_ref.quantize(now[r])
            held.append(decode(q).astype(BF))
            neg = mx_ref.matmul(qu[r], q) + np.float32(0.0) < 0
            key = 4 * B * (cl[r] % A) + 4 * (np.take_along_axis(cl[r], to[r], axis=1) % B) + 2 * neg[::16] + neg[1::16]
            cl[r], one, two = classes(key)
            z = (gcols(held[r], one).astype(np.float32) + gcols(held[r], two).astype(np.float32)) * np.float32(0.5)
            sent.append(mx_ref.quantize(z.astype(BF)))
        for r in range(N):
            e = (r + STEP[t]) % N
            h = tile([np.maximum(mx_ref.matmul(pick(lay[e], np.arange(128 * b, 128 * b + 128)), sent[r]), np.float32(0.0)) * np.float32(0.03125) for b in range(4)])
            came = decode(mx_ref.quantize(h)).astype(BF)
            now[r] = (held[r].astype(np.float32) + gcols(came, cl[r]).astype(np.float32)).astype(BF)
    y, ol = np.zeros((N, 128, C), np.float32), np.zeros((N, 8, C), np.float32)
    oc, osc = np.zeros((N, 128, 4 * C), np.uint8), np.zeros((N, 16, C), np.uint8)
    for r in range(N):
        q = mx_ref.quantize(now[r])
        y[r] = mx_ref.matmul(mx_ref.quantize(v[r]), q)
        ol[r] = cl[r]
        oc[r], osc[r] = emit(q)
    return {"y": y, "ol": ol, "oc": oc, "osc": osc}

@@ -1,0 +1,421 @@
+from concourse.bass import DstId, RemoteDMATransfer
+from concourse.mybir import dt, AluOpType, ActivationFunctionType
+
+C, K, ROUNDS = 192, 64, 3
+STEP = [1, 2, 3]
+PL = 2 * C + K
+EPS = 2048.0
+BIG = 4096.0
+
+X4 = "float8_e4m3fn_x4"
+SCRATCH = {
+    "tt": ("sbuf", [128, 768], "bfloat16"), "ut": ("sbuf", [128, 512], "bfloat16"), "vt": ("sbuf", [128, 512], "bfloat16"),
+    "nxi": ("sbuf", [128, 12], "int32"), "coi": ("sbuf", [128, 12], "int32"),
+    "qw": ("sbuf", [128, 512], X4), "sw": ("sbuf", [128, 512], "uint8"),
+    "qu": ("sbuf", [128, 128], X4), "su": ("sbuf", [128, 128], "uint8"),
+    "qp": ("sbuf", [128, 256], X4), "sp": ("sbuf", [128, 256], "uint8"),
+    "qv": ("sbuf", [128, 128], X4), "sv": ("sbuf", [128, 128], "uint8"),
+    "qt": ("sbuf", [128, 192], X4), "st": ("sbuf", [128, 192], "uint8"),
+    "qe": ("sbuf", [128, 512], X4), "pl": ("sbuf", [128, 768], "uint8"),
+    "qz": ("sbuf", [128, 128], X4), "qh": ("sbuf", [128, 128], X4),
+    "eb": ("sbuf", [128, 520], "bfloat16"), "zh": ("sbuf", [128, 1024], "bfloat16"),
+    "ij": ("sbuf", [128, 128], "float32"), "pi": ("sbuf", [128, 8], "int32"), "col": ("sbuf", [128, 16], "float32"),
+    "m16": ("sbuf", [128, 4], "float32"), "kap": ("sbuf", [128, 4], "float32"), "ini": ("sbuf", [128, 4], "float32"),
+    "uli": ("sbuf", [128, 16], "int32"),
+    "taba": ("sbuf", [128, 64], "bfloat16"), "tabb": ("sbuf", [128, 64], "bfloat16"), "i64": ("sbuf", [128, 64], "bfloat16"),
+    "iw": ("sbuf", [128, PL], "float32"),
+    "tm4": ("sbuf", [128, 64], "bfloat16"), "tm16": ("sbuf", [128, 192], "bfloat16"),
+    "ca": ("sbuf", [128, 192], "bfloat16"), "cb": ("sbuf", [128, 192], "bfloat16"),
+    "cc": ("sbuf", [128, 64], "bfloat16"), "cd": ("sbuf", [128, 64], "bfloat16"),
+    "cw4": ("sbuf", [128, 64], "bfloat16"), "cw16": ("sbuf", [128, 192], "bfloat16"),
+    "ones": ("sbuf", [128, 192], "bfloat16"),
+    "off": ("sbuf", [128, 96], "uint16"),
+    "fb": ("sbuf", [128, 4 * PL], "bfloat16"), "aa": ("sbuf", [128, 256], "bfloat16"), "gg": ("sbuf", [128, 256], "float32"),
+    "dh": ("sbuf", [128, 256], "bfloat16"), "tmp": ("sbuf", [128, 384], "bfloat16"),
+    "ar": ("sbuf", [128, 192], "bfloat16"), "br": ("sbuf", [128, 192], "bfloat16"), "p8": ("sbuf", [128, 192], "bfloat16"),
+    "t1": ("sbuf", [128, 192], "bfloat16"), "t2": ("sbuf", [128, 192], "bfloat16"), "sb": ("sbuf", [128, 192], "bfloat16"),
+    "kk": ("sbuf", [128, 192], "bfloat16"), "d0": ("sbuf", [128, 768], "bfloat16"), "vs": ("sbuf", [128, 768], "float32"),
+    "fr": ("sbuf", [128, 4], "int32"), "dd": ("sbuf", [128, 4], "float32"), "gp": ("sbuf", [128, 4], "float32"),
+    "sx": ("sbuf", [128, 4], "float32"),
+    "rk": ("sbuf", [128, 4], "float32"), "junk": ("sbuf", [128, 256], "bfloat16"),
+    "se": ("sbuf", [128, 64], "bfloat16"), "ses": ("sbuf", [128, 64], "float32"),
+    "rr": ("sbuf", [128, 64], "bfloat16"), "ks": ("sbuf", [128, 192], "float32"),
+    "cr": ("sbuf", [128, 192], "float32"), "cs": ("sbuf", [128, 192], "float32"),
+    "yo": ("sbuf", [128, 192], "float32"),
+}
+for _t in range(ROUNDS):
+    SCRATCH["lc%d" % _t] = ("sbuf", [128, 256], X4)
+    SCRATCH["lp%d" % _t] = ("sbuf", [128, 640], "uint8")
+for _b in ("pa", "pb", "f0", "f1", "f2", "f3", "x0", "x1"):
+    SCRATCH[_b] = ("psum", [128, 512], "float32")
+
+NPOOL, NDMA = 60, 16
+SEMAPHORES = (["c%d" % k for k in range(NPOOL)] + ["d%d" % k for k in range(NDMA)]
+              + ["za%d" % t for t in range(ROUNDS)] + ["ha%d" % t for t in range(ROUNDS)]
+              + ["zl%d" % t for t in range(ROUNDS)] + ["hl%d" % t for t in range(ROUNDS)])
+
+O_F, O_S, O_R, O_E, O_K, O_C, O_NX, O_U = 0, 8, 12, 16, 32, 44, 56, 68
+C_I, C_I1, C_Q, C_Q1, C_M4, C_A4, C_M16, C_M16K = 0, 1, 2, 3, 4, 5, 6, 7
+
+
+def emit(g, T, ops):
+    queue = {"g": g, "v": g.vector, "a": g.scalar, "p": g.tensor, "s": g.sync}
+    last_w, readers, known, members = {}, {}, {q: set() for q in queue}, {}
+    for n, o in enumerate(ops):
+        if o["grp"] is None:
+            o["grp"] = ("own", n)
+        members.setdefault(o["grp"], []).append(n)
+    for n, o in enumerate(ops):
+        deps = set(o["after"])
+        for r in o["r"]:
+            if r in last_w:
+                deps.add(last_w[r])
+            if r.startswith("ps"):
+                deps.update(k for k in readers.get(r, []) if ops[k]["q"] != o["q"])
+        for w in o["w"]:
+            if w in last_w:
+                deps.add(last_w[w])
+            deps.update(readers.get(w, []))
+        deps.discard(n)
+        if o["kind"] != "hoist":
+            for r in o["r"]:
+                readers.setdefault(r, []).append(n)
+            for w in o["w"]:
+                last_w[w] = n
+                readers[w] = []
+        if o["q"] is None:
+            o["know"], o["waits"] = set(), []
+            continue
+        kn = known[o["q"]]
+        deps = sorted(d for d in deps if d not in kn)
+        deps = [d for d in deps if not any(d in ops[e]["know"] for e in deps if e != d)]
+        o["waits"] = []
+        for d in deps:
+            if d in kn:
+                continue
+            o["waits"].append(d)
+            for e in members[ops[d]["grp"]]:
+                assert e < n
+                ops[e]["needed"] = True
+                kn.add(e)
+                kn.update(ops[e]["know"])
+        o["know"] = set(kn)
+    user, count, ndma, given = [[] for k in range(NPOOL)], [0] * NPOOL, [0], {}
+    for n, o in enumerate(ops):
+        if o["q"] is None:
+            continue
+        q = queue[o["q"]]
+        for d in o["waits"]:
+            q.wait_ge(ops[d]["sem"][0], ops[d]["sem"][1])
+        if o["fn"] is None:
+            continue
+        ins = o["fn"]()
+        if o["kind"] == "dma":
+            if o["grp"] not in given:
+                given[o["grp"]] = (T.sem["d%d" % ndma[0]], 16 * len(members[o["grp"]]))
+                ndma[0] += 1
+            o["sem"] = given[o["grp"]]
+            ins.then_inc(o["sem"][0], 16)
+        elif o["kind"] == "op" and o["needed"]:
+            if o["grp"] not in given:
+                mem = members[o["grp"]]
+                k = [j for j in range(NPOOL) if all(u in ops[e]["know"] for u in user[j] for e in mem)][0]
+                user[k] = mem
+                count[k] += len(mem)
+                given[o["grp"]] = (T.sem["c%d" % k], count[k])
+            o["sem"] = given[o["grp"]]
+            ins.then_inc(o["sem"][0], 1)
+
+
+def rank_program(g, core, T, topo):
+    rank = T.rank_of(core)
+    if rank is None:
+        return
+    N = len(T.cores)
+    V, A, P = g.vector, g.scalar, g.tensor
+    Alu, Act = AluOpType, ActivationFunctionType
+    ops = []
+
+    def op(q, fn, r=(), w=(), after=(), kind="op", sem=None):
+        ops.append({"q": q, "fn": fn, "r": list(r), "w": list(w), "after": list(after), "kind": kind, "sem": sem,
+                    "needed": False, "grp": None})
+        return len(ops) - 1
+
+    def group(name, ids):
+        for k in ids:
+            ops[k]["grp"] = name
+
+    def hoist(q, r=(), w=()):
+        op(q, None, r, w, kind="hoist")
+
+    def dma(q, out, in_, r=(), w=(), after=()):
+        e = {"s": g.sync, "a": g.scalar}[q]
+        return op(q, lambda: e.dma_start(out, in_), r, w, after, kind="dma")
+
+    def ts(out, in0, s1, s2, o0, o1, r, w):
+        if o1 is None:
+            return op("v", lambda: V.tensor_scalar(out, in0, s1, None, o0), r, w)
+        return op("v", lambda: V.tensor_scalar(out, in0, s1, s2, o0, o1), r, w)
+
+    def tt(out, a, b, o, r, w):
+        return op("v", lambda: V.tensor_tensor(out, a, b, o), r, w)
+
+    def cp(out, in_, r, w):
+        return op("v", lambda: V.tensor_copy(out, in_), r, w)
+
+    def act(out, in_, f, r, w, **kw):
+        return op("a", lambda: A.activation(out, in_, f, **kw), r, w)
+
+    def quant(q, s, x, r, w):
+        return op("v", lambda: V.quantize_mx(q, s, x), r, w)
+
+    def mm(bank, n, lq, ls, rq, rs, r):
+        return op("p", lambda: P.matmul_mx(T[bank][:, 0:n], lq, ls, rq, rs, True, True), r, ["ps" + bank])
+
+    def scan(out, d0, d1, init, r, w):
+        return op("v", lambda: V.tensor_tensor_scan(out, d0, d1, init, Alu.mult, Alu.add), r, w)
+
+    def iota(out, pat, base, cm, w, small=True):
+        if small:
+            return op("g", lambda: g.iota(out, pat, base, cm, allow_small_or_imprecise_dtypes=True), (), w)
+        return op("g", lambda: g.iota(out, pat, base, cm), (), w)
+
+    def fill(ap, c, w):
+        return op("v", lambda: V.memset(ap, c), (), w)
+
+    def off(o, k):
+        return T.off[:, o:o + k]
+
+    def col(k):
+        return T.col[:, k:k + 1]
+
+    def send(to, codes, plane, lcodes, lplane, rsem, lsem, r):
+        dst = T.cores[to]
+        rid, pid = topo.addr(dst)[:2]
+        eng = topo.engines(core, dst)
+        half = len(eng) // 2
+        masks = [sum(1 << e for e in eng[:half]), sum(1 << e for e in eng[half:])]
+
+        def fn():
+            tr = [RemoteDMATransfer(dst_ids=[DstId(rid=rid, pnc=pid)], dma_engine_mask=masks[0], remote_sem=rsem,
+                                    src=codes.bitcast(dt.uint8), dst=lcodes.bitcast(dt.uint8)),
+                  RemoteDMATransfer(dst_ids=[DstId(rid=rid, pnc=pid)], dma_engine_mask=masks[1], remote_sem=rsem,
+                                    src=plane, dst=lplane)]
+            return g.remote_dma_fused(tr, local_sem=lsem)
+        return op("g", fn, r, (), kind="remote", sem=(lsem, 2 * half))
+
+    def arrival(frm, sem, w):
+        n = len(topo.engines(T.cores[frm], core)) // 2 * 2
+        return op(None, None, (), w, kind="arrival", sem=(sem, n))
+
+    def eq(b):
+        return T.qe[:, 128 * b:128 * b + 128], T.pl[:, 128 + 128 * b:256 + 128 * b]
+
+    def quant_e(b):
+        quant(eq(b)[0], eq(b)[1], T.eb[:, 3 - b:515 - b], ["eb"], ["e%d" % b])
+
+    def prekeys():
+        act(T.ar[:], T.taba[:].indirect(off(O_C, 12)), Act.Copy, ["taba", "oc"], ["ar"], scale=0.25)
+        act(T.br[:], T.tabb[:].indirect(off(O_C, 12)), Act.Copy, ["tabb", "oc"], ["br"], scale=0.125)
+        tt(T.p8[:], T.br[:].indirect(off(O_NX, 12)), T.ar[:], Alu.add, ["br", "ar", "onx"], ["p8"])
+
+    def zero_landing(t):
+        quant(T["lc%d" % t][:, 64:192], T["lp%d" % t][:, 256:384], T.zh[:, 256:768], ["zero"], ["lz%d" % t])
+
+    tplanes = ["t0", "t1p", "t2p", "t3"]
+    ending = []
+
+    lu = dma("s", T.ut[:], T.u[:], (), ["ut"])
+    lx = dma("a", T.tt[:], T.x[:], (), tplanes)
+    dma("a", T.coi[:], T.co[:], (), ["coi"])
+    dma("a", T.nxi[:], T.nx[:], (), ["nxi"])
+    dma("s", T.qw[:].bitcast(dt.uint8), T.wc[:], (), ["qw"], after=[lu, lx])
+    dma("s", T.sw[:], T.ws[:], (), ["sw"])
+    dma("s", T.vt[:], T.v[:], (), ["vt"])
+
+    iota(T.ij[:], [[1, 128]], 0, -1, ["ij"])
+    iota(T.pi[:, 0:1], [[0, 1]], 0, 1, ["pi0"], small=False)
+    iota(T.m16[:], [[16, 4]], 0, 0, ["m16"])
+    iota(T.taba[:], [[0, 8], [1, 8]], 0, 0, ["taba"])
+    iota(T.tabb[:], [[0, 32], [1, 2]], 8, 0, ["tabb"])
+    iota(T.tm4[:], [[0, 16], [1, 4]], 0, 0, ["tm4"])
+    iota(T.uli[:], [[1, 2], [16, 8]], 0, 0, ["uli"], small=False)
+    iota(T.iw[:], [[2, PL]], 3, 0, ["iw"])
+    iota(T.i64[:], [[1, 64]], 0, 0, ["i64"])
+    iota(T.tm16[:], [[0, 12], [1, 16]], 0, 0, ["tm16"])
+
+    fill(T.eb[:], 0.0, ["eb"])
+    fill(T.zh[:, 256:768], 0.0, ["zero"])
+    fill(T.ones[:], 1.0, ["ones"])
+    for b in range(4):
+        fill(T.fb[:, PL * b + 2 * C:PL * b + PL], 0.0, ["fz%d" % b])
+    ts(T.eb[:, 3:515:4], T.ij[:], 0.0, None, Alu.is_equal, None, ["ij"], ["eb"])
+    ts(T.pi[:, 1:2], T.pi[:, 0:1], 15, None, Alu.bitwise_and, None, ["pi0"], ["pi1"])
+    quant_e(0)
+    cp(col(C_I), T.pi[:, 1:2], ["pi1"], ["ci"])
+    ts(T.pi[:, 2:3], T.pi[:, 1:2], 2, None, Alu.arith_shift_right, None, ["pi1"], ["pi2"])
+    ts(T.pi[:, 3:4], T.pi[:, 1:2], 3, None, Alu.bitwise_and, None, ["pi1"], ["pi3"])
+    quant_e(1)
+    cp(off(O_C, 12), T.coi[:], ["coi"], ["oc"])
+    cp(off(O_NX, 12), T.nxi[:], ["nxi"], ["onx"])
+    ts(T.kap[:], T.m16[:], col(C_I), 0.125, Alu.add, Alu.mult, ["m16", "ci"], ["kap"])
+    ts(T.ini[:], T.m16[:], col(C_I), float(C + 1), Alu.add, Alu.add, ["m16", "ci"], ["ini"])
+    cp(col(C_Q), T.pi[:, 2:3], ["pi2"], ["cq"])
+    ts(col(C_Q1), T.pi[:, 2:3], 1.0, None, Alu.add, None, ["pi2"], ["cq1"])
+    ts(col(C_A4), T.pi[:, 3:4], 64.0, 0.1, Alu.mult, Alu.add, ["pi3"], ["ca4"])
+    ts(col(C_M4), T.pi[:, 2:3], 3.0, 1.0 / BIG, Alu.is_equal, Alu.max, ["pi2"], ["cm4"])
+    ts(T.cc[:], T.tm4[:], col(C_Q), None, Alu.not_equal, None, ["tm4", "cq"], ["cc"])
+    ts(T.cd[:], T.tm4[:], col(C_Q1), BIG, Alu.is_equal, Alu.mult, ["tm4", "cq1"], ["cd"])
+    cp(off(O_U, 16), T.uli[:], ["uli"], ["ou"])
+    tt(T.cw4[:], T.cc[:], T.cd[:], Alu.max, ["cc", "cd"], ["cw4"])
+    prekeys()
+    quant(T.qu[:], T.su[:], T.ut[:], ["ut"], ["qu"])
+    op("v", lambda: V.tensor_copy(T.qp[:].bitcast(dt.uint32), T.qu[:].bitcast(dt.uint32).indirect(off(O_U, 16))), ["qu", "ou"], ["qp"])
+    act(T.sp[:], T.su[:].indirect(off(O_U, 16)), Act.Copy, ["qu", "ou"], ["sp"])
+
+    vcol = [T.vs[:, C * m + C - 1:C * m + C] for m in range(4)]
+    vall = T.vs[:, C - 1:4 * C:C]
+    vres = ["vs%d" % m for m in range(4)]
+
+    for t in range(ROUNDS):
+        to, frm = (rank + STEP[t]) % N, (rank - STEP[t]) % N
+        lc, lp = T["lc%d" % t], T["lp%d" % t]
+        quant(T.qt[:], T.st[:], T.tt[:], tplanes, ["qt"])
+        mm("pa", C, T.qp[:, 0:128], T.sp[:, 0:128], T.qt[:], T.st[:], ["qp", "sp", "qt"])
+        mm("pb", C, T.qp[:, 128:256], T.sp[:, 128:256], T.qt[:], T.st[:], ["qp", "sp", "qt"])
+        if t == 0:
+            quant_e(2)
+            quant_e(3)
+        for b in range(4):
+            mm("f%d" % b, C, eq(b)[0], eq(b)[1], T.qt[:], T.st[:], ["e%d" % b, "qt"])
+        ts(T.t1[:], T.pa[:, 0:C], 0.0, 4.0, Alu.is_lt, Alu.mult, ["pspa"], ["k1"])
+        act(T.sb[:], T.pb[:, 0:C], Act.Sign, ["pspb"], ["sb"], bias=2.0 ** -120)
+        for b, h in ((0, 0), (1, 0), (0, 1), (1, 1), (2, 0), (3, 0), (2, 1), (3, 1)):
+            act(T.fb[:, PL * b + C * h:PL * b + C * h + C], T["f%d" % b][:, 0:C], Act.Copy, ["psf%d" % b], ["ff%d%d" % (b, h)])
+        tt(T.t2[:], T.t1[:], T.p8[:], Alu.add, ["k1", "p8"], ["k2"])
+        tt(T.kk[:], T.t2[:], T.sb[:], Alu.subtract, ["k2", "sb"], ["kk"])
+        for m in range(4):
+            ts(T.d0[:, C * m:C * m + C], T.kk[:, ::-1], T.kap[:, m:m + 1], 1.0 / EPS, Alu.not_equal, Alu.max, ["kk", "kap"], ["d0%d" % m])
+        group(("vs", t), [scan(T.vs[:, C * m:C * m + C], T.d0[:, C * m:C * m + C], T.ones[:], T.ini[:, m:m + 1],
+                               ["d0%d" % m, "ones", "ini"], [vres[m]]) for m in range(4)])
+        ts(off(O_F, 4), vall, -0.9, None, Alu.add, None, vres, ["of"])
+        ts(T.fr[:], vall, -1.0, None, Alu.add, None, vres, ["fr"])
+        group(("rk", t), [act(T.junk[:, K * m:K * m + K], T.iw[:].indirect(off(O_F, 4)), Act.Sign, ["iw", "of", vres[m]],
+                              ["rk%d" % m], scale=-0.5, bias=vcol[m], accum_out=T.rk[:, m:m + 1]) for m in range(4)])
+
+        def plane(b):
+            return T.fb[:, PL * b:PL * b + PL], ["ff%d0" % b, "ff%d1" % b, "fz%d" % b]
+
+        def first(b, q):
+            o, w = T.aa[:, K * b:K * b + K], plane(b)[0].indirect(off(O_F, 4))
+            if q == "v":
+                cp(o, w, plane(b)[1] + ["of"], ["fa%d" % b])
+            else:
+                act(o, w, Act.Copy, plane(b)[1] + ["of"], ["fa%d" % b])
+
+        def both(b):
+            return tt(T.gg[:, K * b:K * b + K], plane(b)[0].indirect(off(O_S, 4)), T.aa[:, K * b:K * b + K],
+                      Alu.add, plane(b)[1] + ["fa%d" % b, "os"], ["gg%d" % b])
+
+        tt(T.dd[:], vall, T.fr[:], Alu.subtract, vres + ["fr"], ["dd"])
+        first(0, "v")
+        ts(T.gp[:], T.dd[:], EPS, EPS + C, Alu.mult, Alu.min, ["dd"], ["gp"])
+        first(1, "v")
+        first(2, "a")
+        first(3, "a")
+        tt(T.sx[:], T.gp[:], T.fr[:], Alu.add, ["gp", "fr"], ["sx"])
+        ts(off(O_R, 4), T.rk[:], 0.5, 32.1, Alu.mult, Alu.add, ["rk%d" % m for m in range(4)], ["or"])
+        ts(off(O_S, 4), T.sx[:], 0.1 - EPS, None, Alu.add, None, ["sx"], ["os"])
+        cp(T.se[:].indirect(off(O_R, 4)), T.i64[:], ["or", "i64"], ["se"])
+        ids = [both(0)]
+        scan(T.ses[:], T.cw4[:], T.se[:], 0.0, ["cw4", "se"], ["ses"])
+        ids.append(both(1))
+        ids.append(ts(off(O_E, 16), T.ses[:, 3:K:4], col(C_M4), col(C_A4), Alu.mult, Alu.add, ["ses", "cm4", "ca4"], ["oe"]))
+        ids.append(both(2))
+        ids.append(both(3))
+        group(("gg", t), ids)
+        gres = ["gg%d" % b for b in range(4)]
+        group(("z", t), [
+            act(T.zh[:, 0:128], T.gg[:].indirect(off(O_E, 8)), Act.Copy, gres + ["oe"], ["z0"], scale=0.5),
+            ts(T.zh[:, 128:256], T.gg[:].indirect(off(O_E + 8, 8)), 0.5, None, Alu.mult, None, gres + ["oe"], ["z1"])])
+        quant(T.qz[:], T.pl[:, 640:768], T.zh[:, 0:512], ["z0", "z1", "zero"], ["qz"])
+        ending.append(send(to, T.qz[:, 0:64], T.pl[:, 448:704], lc[:, 0:64], lp[:, 0:256],
+                           T.sem["za%d" % t], T.sem["zl%d" % t], ["qz", "e2", "e3"]))
+
+        act(T.rr[:], T.i64[:].indirect(off(O_R, 4)), Act.Copy, ["i64", "or"], ["rr"])
+        if t == 0:
+            zero_landing(0)
+            ts(col(C_I1), col(C_I), 1.0, None, Alu.add, None, ["ci"], ["ci1"])
+            ts(col(C_M16), col(C_I), 15.0, 1.0 / BIG, Alu.is_equal, Alu.max, ["ci"], ["cm16"])
+            ts(T.ca[:], T.tm16[:], col(C_I), None, Alu.not_equal, None, ["tm16", "ci"], ["ca"])
+            ts(T.cb[:], T.tm16[:], col(C_I1), BIG, Alu.is_equal, Alu.mult, ["tm16", "ci1"], ["cb"])
+            ts(col(C_M16K), col(C_M16), 8.0, None, Alu.mult, None, ["cm16"], ["cm16k"])
+            tt(T.cw16[:], T.ca[:], T.cb[:], Alu.max, ["ca", "cb"], ["cw16"])
+        scan(T.ks[:], T.cw16[:], T.kk[:], 0.0, ["cw16", "kk"], ["ks"])
+        ts(off(O_K, 12), T.ks[:, 15:C:16], col(C_M16K), 0.1, Alu.mult, Alu.add, ["ks", "cm16k"], ["ok"])
+        cp(T.cr[:], T.rr[:].indirect(off(O_K, 12)), ["rr", "ok"], ["cr"])
+        if t == ROUNDS - 1:
+            ids = [dma("s", T.ol[gi:gi + 1, :], T.cr[16 * gi:16 * gi + 1, :], ["cr"], ()) for gi in range(8)]
+            group("ol", ids)
+            ending.extend(ids)
+
+        wb = ["pa", "pb", "x0", "x1"]
+        hoist("v", (), ["qh", "h1", "h3"])
+        hoist("a", (), ["h0", "h2"])
+        hoist("p", ["qw", "sw", "lz%d" % t], ["ps" + b for b in wb])
+        arrival(frm, T.sem["za%d" % t], ["lza%d" % t])
+        for b in range(4):
+            mm(wb[b], 128, T.qw[:, 128 * b:128 * b + 128], T.sw[:, 128 * b:128 * b + 128], lc[:, 0:128], lp[:, 192:320],
+               ["qw", "sw", "lza%d" % t, "lz%d" % t])
+        ids = []
+        for b in range(4):
+            o, i = T.zh[:, 768 + b:1024:4], T[wb[b]][:, 0:K]
+            if b % 2 == 0:
+                ids.append(act(o, i, Act.Relu, ["ps" + wb[b]], ["h%d" % b], scale=0.03125))
+            else:
+                ids.append(ts(o, i, 0.0, 0.03125, Alu.max, Alu.mult, ["ps" + wb[b]], ["h%d" % b]))
+        group(("h", t), ids)
+        quant(T.qh[:], T.pl[:, 0:128], T.zh[:, 512:1024], ["h0", "h1", "h2", "h3", "zero"], ["qh"])
+        ending.append(send(frm, T.qh[:, 64:128], T.pl[:, 64:320], lc[:, 192:256], lp[:, 384:640],
+                           T.sem["ha%d" % t], T.sem["hl%d" % t], ["qh", "e0", "e1"]))
+
+        scan(T.cs[:], T.cw16[:], T.cr[:], 0.0, ["cw16", "cr"], ["cs"])
+        ts(off(O_C, 12), T.cs[:, 15:C:16], col(C_M16), 0.1, Alu.mult, Alu.add, ["cs", "cm16"], ["oc"])
+        if t < ROUNDS - 1:
+            zero_landing(t + 1)
+            prekeys()
+        else:
+            quant(T.qv[:], T.sv[:], T.vt[:], ["vt"], ["qv"])
+
+        db = ["x0", "x1", "pa", "pb"]
+        hoist("v", (), ["qz", "z1", "qt", "dh0"] + tplanes)
+        hoist("a", ["oc"], ["z0", "dh1", "dh2", "dh3", "tmp2", "tmp3"])
+        hoist("p", (), ["ps" + b for b in db])
+        arrival(to, T.sem["ha%d" % t], ["lha%d" % t])
+        for b in range(4):
+            mm(db[b], 128, eq(b)[0], eq(b)[1], lc[:, 128:256], lp[:, 320:448], ["e%d" % b, "lha%d" % t, "lz%d" % t])
+
+        def dwin(b):
+            return T.dh[:, K * b:K * b + K]
+
+        cp(dwin(0), T[db[0]][:, K:2 * K], ["ps" + db[0]], ["dh0"])
+        act(dwin(1), T[db[1]][:, K:2 * K], Act.Copy, ["ps" + db[1]], ["dh1"])
+        for b in (2, 3):
+            act(dwin(b), T[db[b]][:, K:2 * K], Act.Copy, ["ps" + db[b]], ["dh%d" % b])
+            act(T.tmp[:, C * (b - 2):C * (b - 1)], dwin(b).indirect(off(O_C, 12)), Act.Copy, ["dh%d" % b, "oc"], ["tmp%d" % b])
+        ids = [tt(T.tt[:, b:4 * C:4], dwin(b).indirect(off(O_C, 12)), T.fb[:, PL * b:PL * b + C], Alu.add,
+                  ["dh%d" % b, "oc", "ff%d0" % b], [tplanes[b]]) for b in (0, 1)]
+        ids += [tt(T.tt[:, b:4 * C:4], T["f%d" % b][:, 0:C], T.tmp[:, C * (b - 2):C * (b - 1)], Alu.add,
+                   ["psf%d" % b, "tmp%d" % b], [tplanes[b]]) for b in (2, 3)]
+        group(("t", t), ids)
+
+    quant(T.qt[:], T.st[:], T.tt[:], tplanes, ["qt"])
+    mm("x0", C, T.qv[:], T.sv[:], T.qt[:], T.st[:], ["qv", "qt"])
+    ending.append(dma("s", T.oc[:], T.qt[:].bitcast(dt.uint8), ["qt"], ()))
+    ids = [dma("a", T.osc[4 * k:4 * k + 4, :], T.st[32 * k:32 * k + 4, :], ["qt"], ()) for k in range(4)]
+    group("osc", ids)
+    ending.extend(ids)
+    cp(T.yo[:], T.x0[:, 0:C], ["psx0"], ["yo"])
+    ending.append(dma("s", T.y[:], T.yo[:], ["yo"], ()))
+    op("g", None, (), (), after=ending)
+    emit(g, T, ops)

@@ -3,9 +3,10 @@ from concourse.mybir import dt, AluOpType, ActivationFunctionType
 
 C, K, ROUNDS = 192, 64, 3
 STEP = [1, 2, 3]
-PL = 2 * C + K
-EPS = 2048.0
+PL = C + K
+PS = 200
 BIG = 4096.0
+FAR = 256.0
 
 X4 = "float8_e4m3fn_x4"
 SCRATCH = {
@@ -16,46 +17,47 @@ SCRATCH = {
     "qp": ("sbuf", [128, 256], X4), "sp": ("sbuf", [128, 256], "uint8"),
     "qv": ("sbuf", [128, 128], X4), "sv": ("sbuf", [128, 128], "uint8"),
     "qt": ("sbuf", [128, 192], X4), "st": ("sbuf", [128, 192], "uint8"),
-    "qe": ("sbuf", [128, 512], X4), "pl": ("sbuf", [128, 768], "uint8"),
-    "qz": ("sbuf", [128, 128], X4), "qh": ("sbuf", [128, 128], X4),
-    "eb": ("sbuf", [128, 520], "bfloat16"), "zh": ("sbuf", [128, 1024], "bfloat16"),
+    "qe": ("sbuf", [128, 512], X4), "pl": ("sbuf", [128, 640], "uint8"),
+    "qz": ("sbuf", [128, 128], X4), "sz": ("sbuf", [128, 128], "uint8"), "qh": ("sbuf", [128, 128], X4),
+    "eb": ("sbuf", [128, 520], "bfloat16"), "zh": ("sbuf", [128, 768], "bfloat16"),
     "ij": ("sbuf", [128, 128], "float32"), "pi": ("sbuf", [128, 8], "int32"), "col": ("sbuf", [128, 16], "float32"),
-    "m16": ("sbuf", [128, 4], "float32"), "kap": ("sbuf", [128, 4], "float32"), "ini": ("sbuf", [128, 4], "float32"),
+    "m16": ("sbuf", [128, 4], "float32"), "kap": ("sbuf", [128, 4], "float32"), "kab": ("sbuf", [128, 4], "float32"),
     "uli": ("sbuf", [128, 16], "int32"),
     "taba": ("sbuf", [128, 64], "bfloat16"), "tabb": ("sbuf", [128, 64], "bfloat16"), "i64": ("sbuf", [128, 64], "bfloat16"),
-    "iw": ("sbuf", [128, PL], "float32"),
-    "tm4": ("sbuf", [128, 64], "bfloat16"), "tm16": ("sbuf", [128, 192], "bfloat16"),
+    "iw": ("sbuf", [128, PL], "float32"), "jr": ("sbuf", [128, C], "bfloat16"),
+    "tm8": ("sbuf", [128, 64], "bfloat16"), "tm16": ("sbuf", [128, 192], "bfloat16"),
     "ca": ("sbuf", [128, 192], "bfloat16"), "cb": ("sbuf", [128, 192], "bfloat16"),
     "cc": ("sbuf", [128, 64], "bfloat16"), "cd": ("sbuf", [128, 64], "bfloat16"),
-    "cw4": ("sbuf", [128, 64], "bfloat16"), "cw16": ("sbuf", [128, 192], "bfloat16"),
-    "ones": ("sbuf", [128, 192], "bfloat16"),
-    "off": ("sbuf", [128, 96], "uint16"),
-    "fb": ("sbuf", [128, 4 * PL], "bfloat16"), "aa": ("sbuf", [128, 256], "bfloat16"), "gg": ("sbuf", [128, 256], "float32"),
+    "cw8": ("sbuf", [128, 64], "bfloat16"), "cw16": ("sbuf", [128, 192], "bfloat16"),
+    "off": ("sbuf", [128, 64], "uint16"), "ms": ("sbuf", [128, 16], "uint16"),
+    "fh": ("sbuf", [128, 4 * PL], "bfloat16"), "fb": ("sbuf", [128, 2 * C], "bfloat16"),
+    "aa": ("sbuf", [128, 256], "bfloat16"), "gg": ("sbuf", [128, 256], "float32"),
     "dh": ("sbuf", [128, 256], "bfloat16"), "tmp": ("sbuf", [128, 384], "bfloat16"),
     "ar": ("sbuf", [128, 192], "bfloat16"), "br": ("sbuf", [128, 192], "bfloat16"), "p8": ("sbuf", [128, 192], "bfloat16"),
     "t1": ("sbuf", [128, 192], "bfloat16"), "t2": ("sbuf", [128, 192], "bfloat16"), "sb": ("sbuf", [128, 192], "bfloat16"),
-    "kk": ("sbuf", [128, 192], "bfloat16"), "d0": ("sbuf", [128, 768], "bfloat16"), "vs": ("sbuf", [128, 768], "float32"),
-    "fr": ("sbuf", [128, 4], "int32"), "dd": ("sbuf", [128, 4], "float32"), "gp": ("sbuf", [128, 4], "float32"),
-    "sx": ("sbuf", [128, 4], "float32"),
-    "rk": ("sbuf", [128, 4], "float32"), "junk": ("sbuf", [128, 256], "bfloat16"),
+    "kk": ("sbuf", [128, 192], "bfloat16"), "d0": ("sbuf", [128, 768], "bfloat16"),
+    "p1": ("sbuf", [128, 4 * PS], "bfloat16"), "p2": ("sbuf", [128, 4 * C], "bfloat16"),
+    "tl": ("sbuf", [128, 4], "float32"), "rk": ("sbuf", [128, 4], "float32"), "junk": ("sbuf", [128, 256], "bfloat16"),
     "se": ("sbuf", [128, 64], "bfloat16"), "ses": ("sbuf", [128, 64], "float32"),
     "rr": ("sbuf", [128, 64], "bfloat16"), "ks": ("sbuf", [128, 192], "float32"),
     "cr": ("sbuf", [128, 192], "float32"), "cs": ("sbuf", [128, 192], "float32"),
     "yo": ("sbuf", [128, 192], "float32"),
 }
 for _t in range(ROUNDS):
-    SCRATCH["lc%d" % _t] = ("sbuf", [128, 256], X4)
-    SCRATCH["lp%d" % _t] = ("sbuf", [128, 640], "uint8")
+    SCRATCH["lc%d" % _t] = ("sbuf", [128, C + K], X4)
+    SCRATCH["lp%d" % _t] = ("sbuf", [128, C + 4 * K], "uint8")
+    SCRATCH["ml%d" % _t] = ("sbuf", [128, 16], "uint16")
 for _b in ("pa", "pb", "f0", "f1", "f2", "f3", "x0", "x1"):
     SCRATCH[_b] = ("psum", [128, 512], "float32")
 
 NPOOL, NDMA = 60, 16
+KINDS = ("t", "m", "e", "h")
 SEMAPHORES = (["c%d" % k for k in range(NPOOL)] + ["d%d" % k for k in range(NDMA)]
-              + ["za%d" % t for t in range(ROUNDS)] + ["ha%d" % t for t in range(ROUNDS)]
-              + ["zl%d" % t for t in range(ROUNDS)] + ["hl%d" % t for t in range(ROUNDS)])
+              + ["%s%s%d" % (k, s, t) for k in KINDS for s in "al" for t in range(ROUNDS)])
 
-O_F, O_S, O_R, O_E, O_K, O_C, O_NX, O_U = 0, 8, 12, 16, 32, 44, 56, 68
-C_I, C_I1, C_Q, C_Q1, C_M4, C_A4, C_M16, C_M16K = 0, 1, 2, 3, 4, 5, 6, 7
+O_R, O_K, O_C, O_NX, O_U = 0, 4, 16, 28, 40
+M_F, M_S, M_E = 0, 4, 8
+C_I, C_I1, C_Q, C_Q1, C_M8, C_A8, C_M16, C_M16K = 0, 1, 2, 3, 4, 5, 6, 7
 
 
 def emit(g, T, ops):
@@ -172,8 +174,8 @@ def rank_program(g, core, T, topo):
     def mm(bank, n, lq, ls, rq, rs, r):
         return op("p", lambda: P.matmul_mx(T[bank][:, 0:n], lq, ls, rq, rs, True, True), r, ["ps" + bank])
 
-    def scan(out, d0, d1, init, r, w):
-        return op("v", lambda: V.tensor_tensor_scan(out, d0, d1, init, Alu.mult, Alu.add), r, w)
+    def scan(out, d0, d1, init, o0, o1, r, w):
+        return op("v", lambda: V.tensor_tensor_scan(out, d0, d1, init, o0, o1), r, w)
 
     def iota(out, pat, base, cm, w, small=True):
         if small:
@@ -189,24 +191,26 @@ def rank_program(g, core, T, topo):
     def col(k):
         return T.col[:, k:k + 1]
 
-    def send(to, codes, plane, lcodes, lplane, rsem, lsem, r):
+    def send(to, calls, name, r):
         dst = T.cores[to]
         rid, pid = topo.addr(dst)[:2]
         eng = topo.engines(core, dst)
-        half = len(eng) // 2
-        masks = [sum(1 << e for e in eng[:half]), sum(1 << e for e in eng[half:])]
+        rsem, lsem = T.sem[name[0] + "a" + name[1:]], T.sem[name[0] + "l" + name[1:]]
 
         def fn():
-            tr = [RemoteDMATransfer(dst_ids=[DstId(rid=rid, pnc=pid)], dma_engine_mask=masks[0], remote_sem=rsem,
-                                    src=codes.bitcast(dt.uint8), dst=lcodes.bitcast(dt.uint8)),
-                  RemoteDMATransfer(dst_ids=[DstId(rid=rid, pnc=pid)], dma_engine_mask=masks[1], remote_sem=rsem,
-                                    src=plane, dst=lplane)]
-            return g.remote_dma_fused(tr, local_sem=lsem)
-        return op("g", fn, r, (), kind="remote", sem=(lsem, 2 * half))
+            for pairs in calls:
+                n = len(eng) // len(pairs)
+                g.remote_dma_fused([RemoteDMATransfer(dst_ids=[DstId(rid=rid, pnc=pid)], remote_sem=rsem, src=s, dst=d,
+                                                      dma_engine_mask=sum(1 << e for e in eng[n * k:n * k + n]))
+                                    for k, (s, d) in enumerate(pairs)], local_sem=lsem)
+        return op("g", fn, r, (), kind="remote", sem=(lsem, len(eng) * len(calls)))
 
-    def arrival(frm, sem, w):
-        n = len(topo.engines(T.cores[frm], core)) // 2 * 2
-        return op(None, None, (), w, kind="arrival", sem=(sem, n))
+    def arrival(frm, name, ncalls, w):
+        n = len(topo.engines(T.cores[frm], core)) * ncalls
+        return op(None, None, (), w, kind="arrival", sem=(T.sem[name[0] + "a" + name[1:]], n))
+
+    def u8(v):
+        return v.bitcast(dt.uint8)
 
     def eq(b):
         return T.qe[:, 128 * b:128 * b + 128], T.pl[:, 128 + 128 * b:256 + 128 * b]
@@ -214,204 +218,222 @@ def rank_program(g, core, T, topo):
     def quant_e(b):
         quant(eq(b)[0], eq(b)[1], T.eb[:, 3 - b:515 - b], ["eb"], ["e%d" % b])
 
-    def prekeys():
-        act(T.ar[:], T.taba[:].indirect(off(O_C, 12)), Act.Copy, ["taba", "oc"], ["ar"], scale=0.25)
+    def pre_rows():
         act(T.br[:], T.tabb[:].indirect(off(O_C, 12)), Act.Copy, ["tabb", "oc"], ["br"], scale=0.125)
-        tt(T.p8[:], T.br[:].indirect(off(O_NX, 12)), T.ar[:], Alu.add, ["br", "ar", "onx"], ["p8"])
+        act(T.ar[:], T.taba[:].indirect(off(O_C, 12)), Act.Copy, ["taba", "oc"], ["ar"], scale=0.25)
 
-    def zero_landing(t):
-        quant(T["lc%d" % t][:, 64:192], T["lp%d" % t][:, 256:384], T.zh[:, 256:768], ["zero"], ["lz%d" % t])
+    def pre_keys():
+        tt(T.p8[:], T.br[:].indirect(off(O_NX, 12)), T.ar[:], Alu.add, ["br", "ar", "onx"], ["p8"])
 
     tplanes = ["t0", "t1p", "t2p", "t3"]
     ending = []
 
+    dma("a", T.coi[:], T.co[:], (), ["coi"])
     lu = dma("s", T.ut[:], T.u[:], (), ["ut"])
     lx = dma("a", T.tt[:], T.x[:], (), tplanes)
-    dma("a", T.coi[:], T.co[:], (), ["coi"])
-    dma("a", T.nxi[:], T.nx[:], (), ["nxi"])
-    dma("s", T.qw[:].bitcast(dt.uint8), T.wc[:], (), ["qw"], after=[lu, lx])
+    dma("s", T.nxi[:], T.nx[:], (), ["nxi"])
+    dma("s", u8(T.qw[:]), T.wc[:], (), ["qw"], after=[lu, lx])
     dma("s", T.sw[:], T.ws[:], (), ["sw"])
-    dma("s", T.vt[:], T.v[:], (), ["vt"])
 
-    iota(T.ij[:], [[1, 128]], 0, -1, ["ij"])
     iota(T.pi[:, 0:1], [[0, 1]], 0, 1, ["pi0"], small=False)
-    iota(T.m16[:], [[16, 4]], 0, 0, ["m16"])
-    iota(T.taba[:], [[0, 8], [1, 8]], 0, 0, ["taba"])
-    iota(T.tabb[:], [[0, 32], [1, 2]], 8, 0, ["tabb"])
-    iota(T.tm4[:], [[0, 16], [1, 4]], 0, 0, ["tm4"])
     iota(T.uli[:], [[1, 2], [16, 8]], 0, 0, ["uli"], small=False)
-    iota(T.iw[:], [[2, PL]], 3, 0, ["iw"])
+    iota(T.tabb[:], [[0, 32], [1, 2]], 8, 0, ["tabb"])
+    iota(T.taba[:], [[0, 8], [1, 8]], 0, 0, ["taba"])
+    iota(T.ij[:], [[1, 128]], 0, -1, ["ij"])
+    iota(T.m16[:], [[16, 4]], 0, 0, ["m16"])
+    iota(T.tm8[:], [[0, 8], [1, 8]], 0, 0, ["tm8"])
+    iota(T.jr[:], [[-1, C]], C - 1, 0, ["jr"])
+    iota(T.iw[:], [[2, PL]], 1, 0, ["iw"])
     iota(T.i64[:], [[1, 64]], 0, 0, ["i64"])
     iota(T.tm16[:], [[0, 12], [1, 16]], 0, 0, ["tm16"])
 
+    pini = [T.p1[:, PS * m:PS * m + 1] for m in range(4)]
     fill(T.eb[:], 0.0, ["eb"])
-    fill(T.zh[:, 256:768], 0.0, ["zero"])
-    fill(T.ones[:], 1.0, ["ones"])
-    for b in range(4):
-        fill(T.fb[:, PL * b + 2 * C:PL * b + PL], 0.0, ["fz%d" % b])
-    ts(T.eb[:, 3:515:4], T.ij[:], 0.0, None, Alu.is_equal, None, ["ij"], ["eb"])
+    fill(T.zh[:, 256:512], 0.0, ["zero"])
     ts(T.pi[:, 1:2], T.pi[:, 0:1], 15, None, Alu.bitwise_and, None, ["pi0"], ["pi1"])
-    quant_e(0)
+    for b in range(4):
+        fill(T.fh[:, PL * b + C:PL * b + PL], 0.0, ["fz%d" % b])
     cp(col(C_I), T.pi[:, 1:2], ["pi1"], ["ci"])
-    ts(T.pi[:, 2:3], T.pi[:, 1:2], 2, None, Alu.arith_shift_right, None, ["pi1"], ["pi2"])
-    ts(T.pi[:, 3:4], T.pi[:, 1:2], 3, None, Alu.bitwise_and, None, ["pi1"], ["pi3"])
-    quant_e(1)
-    cp(off(O_C, 12), T.coi[:], ["coi"], ["oc"])
-    cp(off(O_NX, 12), T.nxi[:], ["nxi"], ["onx"])
-    ts(T.kap[:], T.m16[:], col(C_I), 0.125, Alu.add, Alu.mult, ["m16", "ci"], ["kap"])
-    ts(T.ini[:], T.m16[:], col(C_I), float(C + 1), Alu.add, Alu.add, ["m16", "ci"], ["ini"])
+    ts(T.pi[:, 2:3], T.pi[:, 1:2], 1, None, Alu.arith_shift_right, None, ["pi1"], ["pi2"])
+    ts(T.pi[:, 3:4], T.pi[:, 1:2], 1, None, Alu.bitwise_and, None, ["pi1"], ["pi3"])
+    cp(off(O_U, 16), T.uli[:], ["uli"], ["ou"])
     cp(col(C_Q), T.pi[:, 2:3], ["pi2"], ["cq"])
     ts(col(C_Q1), T.pi[:, 2:3], 1.0, None, Alu.add, None, ["pi2"], ["cq1"])
-    ts(col(C_A4), T.pi[:, 3:4], 64.0, 0.1, Alu.mult, Alu.add, ["pi3"], ["ca4"])
-    ts(col(C_M4), T.pi[:, 2:3], 3.0, 1.0 / BIG, Alu.is_equal, Alu.max, ["pi2"], ["cm4"])
-    ts(T.cc[:], T.tm4[:], col(C_Q), None, Alu.not_equal, None, ["tm4", "cq"], ["cc"])
-    ts(T.cd[:], T.tm4[:], col(C_Q1), BIG, Alu.is_equal, Alu.mult, ["tm4", "cq1"], ["cd"])
-    cp(off(O_U, 16), T.uli[:], ["uli"], ["ou"])
-    tt(T.cw4[:], T.cc[:], T.cd[:], Alu.max, ["cc", "cd"], ["cw4"])
-    prekeys()
+    ts(col(C_A8), T.pi[:, 3:4], float(K), 0.1, Alu.mult, Alu.add, ["pi3"], ["ca8"])
+    ts(col(C_M8), T.pi[:, 2:3], 7.0, 1.0 / BIG, Alu.is_equal, Alu.max, ["pi2"], ["cm8"])
+    ts(T.eb[:, 3:515:4], T.ij[:], 0.0, None, Alu.is_equal, None, ["ij"], ["eb"])
+    ts(T.kap[:], T.m16[:], col(C_I), 0.125, Alu.add, Alu.mult, ["m16", "ci"], ["kap"])
+    ts(T.kab[:], T.m16[:], col(C_I), -FAR, Alu.add, Alu.mult, ["m16", "ci"], ["kab"])
+    ts(T.p1[:, 0:4 * PS:PS], T.m16[:], col(C_I), float(C), Alu.add, Alu.add, ["m16", "ci"], ["ini"])
+    quant_e(0)
+    quant_e(1)
+    cp(off(O_C, 12), T.coi[:], ["coi"], ["oc"])
+    pre_rows()
+    quant_e(2)
+    quant_e(3)
     quant(T.qu[:], T.su[:], T.ut[:], ["ut"], ["qu"])
-    op("v", lambda: V.tensor_copy(T.qp[:].bitcast(dt.uint32), T.qu[:].bitcast(dt.uint32).indirect(off(O_U, 16))), ["qu", "ou"], ["qp"])
-    act(T.sp[:], T.su[:].indirect(off(O_U, 16)), Act.Copy, ["qu", "ou"], ["sp"])
+    cp(off(O_NX, 12), T.nxi[:], ["nxi"], ["onx"])
 
-    vcol = [T.vs[:, C * m + C - 1:C * m + C] for m in range(4)]
-    vall = T.vs[:, C - 1:4 * C:C]
-    vres = ["vs%d" % m for m in range(4)]
+    def pick(h):
+        o = off(O_U + 8 * h, 8)
+        s = slice(128 * h, 128 * h + 128)
+        op("v", lambda: V.tensor_copy(T.qp[:, s].bitcast(dt.uint32), T.qu[:].bitcast(dt.uint32).indirect(o)), ["qu", "ou"], ["qp%d" % h])
+        act(T.sp[:, s], T.su[:].indirect(o), Act.Copy, ["qu", "ou"], ["sp%d" % h])
+
+    pick(0)
+
+    first = [T.p1[:, PS * m + C:PS * m + C + 1] for m in range(4)]
+    second = [T.p2[:, C * m + C - 1:C * m + C] for m in range(4)]
+    fres, sres = ["p1%d" % m for m in range(4)], ["p2%d" % m for m in range(4)]
+    slot = [0, 2, 1, 3]
 
     for t in range(ROUNDS):
         to, frm = (rank + STEP[t]) % N, (rank - STEP[t]) % N
-        lc, lp = T["lc%d" % t], T["lp%d" % t]
+        lc, lp, ml = T["lc%d" % t], T["lp%d" % t], T["ml%d" % t]
         quant(T.qt[:], T.st[:], T.tt[:], tplanes, ["qt"])
-        mm("pa", C, T.qp[:, 0:128], T.sp[:, 0:128], T.qt[:], T.st[:], ["qp", "sp", "qt"])
-        mm("pb", C, T.qp[:, 128:256], T.sp[:, 128:256], T.qt[:], T.st[:], ["qp", "sp", "qt"])
+        ending.append(send(to, [[(u8(T.qt[:]), u8(lc[:, 0:C]))], [(T.st[:], lp[:, 0:C])]], "t%d" % t, ["qt"]))
+        mm("pa", C, T.qp[:, 0:128], T.sp[:, 0:128], T.qt[:], T.st[:], ["qp0", "sp0", "qt"])
         if t == 0:
-            quant_e(2)
-            quant_e(3)
+            pick(1)
+            pre_keys()
+        mm("pb", C, T.qp[:, 128:256], T.sp[:, 128:256], T.qt[:], T.st[:], ["qp1", "sp1", "qt"])
+        arrival(frm, "t%d" % t, 2, ["lt%d" % t])
         for b in range(4):
-            mm("f%d" % b, C, eq(b)[0], eq(b)[1], T.qt[:], T.st[:], ["e%d" % b, "qt"])
+            mm("f%d" % b, C, eq(b)[0], eq(b)[1], lc[:, 0:C], lp[:, 0:C], ["e%d" % b, "lt%d" % t])
         ts(T.t1[:], T.pa[:, 0:C], 0.0, 4.0, Alu.is_lt, Alu.mult, ["pspa"], ["k1"])
         act(T.sb[:], T.pb[:, 0:C], Act.Sign, ["pspb"], ["sb"], bias=2.0 ** -120)
-        for b, h in ((0, 0), (1, 0), (0, 1), (1, 1), (2, 0), (3, 0), (2, 1), (3, 1)):
-            act(T.fb[:, PL * b + C * h:PL * b + C * h + C], T["f%d" % b][:, 0:C], Act.Copy, ["psf%d" % b], ["ff%d%d" % (b, h)])
         tt(T.t2[:], T.t1[:], T.p8[:], Alu.add, ["k1", "p8"], ["k2"])
         tt(T.kk[:], T.t2[:], T.sb[:], Alu.subtract, ["k2", "sb"], ["kk"])
-        for m in range(4):
-            ts(T.d0[:, C * m:C * m + C], T.kk[:, ::-1], T.kap[:, m:m + 1], 1.0 / EPS, Alu.not_equal, Alu.max, ["kk", "kap"], ["d0%d" % m])
-        group(("vs", t), [scan(T.vs[:, C * m:C * m + C], T.d0[:, C * m:C * m + C], T.ones[:], T.ini[:, m:m + 1],
-                               ["d0%d" % m, "ones", "ini"], [vres[m]]) for m in range(4)])
-        ts(off(O_F, 4), vall, -0.9, None, Alu.add, None, vres, ["of"])
-        ts(T.fr[:], vall, -1.0, None, Alu.add, None, vres, ["fr"])
-        group(("rk", t), [act(T.junk[:, K * m:K * m + K], T.iw[:].indirect(off(O_F, 4)), Act.Sign, ["iw", "of", vres[m]],
-                              ["rk%d" % m], scale=-0.5, bias=vcol[m], accum_out=T.rk[:, m:m + 1]) for m in range(4)])
 
-        def plane(b):
-            return T.fb[:, PL * b:PL * b + PL], ["ff%d0" % b, "ff%d1" % b, "fz%d" % b]
+        def dm(m):
+            return T.d0[:, C * m:C * m + C]
 
-        def first(b, q):
-            o, w = T.aa[:, K * b:K * b + K], plane(b)[0].indirect(off(O_F, 4))
-            if q == "v":
-                cp(o, w, plane(b)[1] + ["of"], ["fa%d" % b])
-            else:
-                act(o, w, Act.Copy, plane(b)[1] + ["of"], ["fa%d" % b])
-
-        def both(b):
-            return tt(T.gg[:, K * b:K * b + K], plane(b)[0].indirect(off(O_S, 4)), T.aa[:, K * b:K * b + K],
-                      Alu.add, plane(b)[1] + ["fa%d" % b, "os"], ["gg%d" % b])
-
-        tt(T.dd[:], vall, T.fr[:], Alu.subtract, vres + ["fr"], ["dd"])
-        first(0, "v")
-        ts(T.gp[:], T.dd[:], EPS, EPS + C, Alu.mult, Alu.min, ["dd"], ["gp"])
-        first(1, "v")
-        first(2, "a")
-        first(3, "a")
-        tt(T.sx[:], T.gp[:], T.fr[:], Alu.add, ["gp", "fr"], ["sx"])
+        act(dm(3), T.kk[:, ::-1], Act.Abs, ["kk", "kab"], ["d03"], scale=8.0 * FAR, bias=T.kab[:, 3:4])
+        for m in range(3):
+            ts(dm(m), T.kk[:, ::-1], T.kap[:, m:m + 1], FAR, Alu.not_equal, Alu.mult, ["kk", "kap"], ["d0%d" % m])
+        group(("p1", t), [scan(T.p1[:, PS * m + 1:PS * m + 1 + C], dm(m), T.jr[:], pini[m], Alu.min, Alu.max,
+                               ["d0%d" % m, "jr", "ini"], [fres[m]]) for m in range(4)])
+        ts(T.ms[:, M_F:M_F + 4], T.p1[:, C:4 * PS:PS], 0.1, None, Alu.add, None, fres, ["of"])
+        group(("rk", t), [act(T.junk[:, K * m:K * m + K], T.iw[:].indirect(T.ms[:, M_F:M_F + 4]), Act.Sign, ["iw", "of", fres[m]],
+                              ["rk%d" % m], scale=-0.5, bias=first[m], accum_out=T.rk[:, m:m + 1]) for m in range(4)])
+        group(("p2", t), [scan(T.p2[:, C * m:C * m + C], dm(m), T.p1[:, PS * m:PS * m + C], pini[m], Alu.min, Alu.max,
+                               ["d0%d" % m, fres[m], "ini"], [sres[m]]) for m in range(4)])
+        if t == 0:
+            ts(T.cc[:], T.tm8[:], col(C_Q), None, Alu.not_equal, None, ["tm8", "cq"], ["cc"])
+            ts(T.cd[:], T.tm8[:], col(C_Q1), BIG, Alu.is_equal, Alu.mult, ["tm8", "cq1"], ["cd"])
+        ts(T.tl[:], T.p2[:, C - 1:4 * C:C], C - 0.5, 4 * FAR, Alu.is_lt, Alu.mult, sres, ["tl"])
+        if t == 0:
+            tt(T.cw8[:], T.cc[:], T.cd[:], Alu.max, ["cc", "cd"], ["cw8"])
+        group(("os", t), [ts(T.ms[:, M_S + m:M_S + m + 1], T.tl[:, m:m + 1], first[m], second[m], Alu.add, Alu.min,
+                             ["tl", fres[m], sres[m]], ["os%d" % m]) for m in range(4)])
+        ending.append(send(to, [[(T.ms[:, 0:8], ml[:, 0:8])]], "m%d" % t, ["of"] + ["os%d" % m for m in range(4)]))
         ts(off(O_R, 4), T.rk[:], 0.5, 32.1, Alu.mult, Alu.add, ["rk%d" % m for m in range(4)], ["or"])
-        ts(off(O_S, 4), T.sx[:], 0.1 - EPS, None, Alu.add, None, ["sx"], ["os"])
         cp(T.se[:].indirect(off(O_R, 4)), T.i64[:], ["or", "i64"], ["se"])
-        ids = [both(0)]
-        scan(T.ses[:], T.cw4[:], T.se[:], 0.0, ["cw4", "se"], ["ses"])
-        ids.append(both(1))
-        ids.append(ts(off(O_E, 16), T.ses[:, 3:K:4], col(C_M4), col(C_A4), Alu.mult, Alu.add, ["ses", "cm4", "ca4"], ["oe"]))
-        ids.append(both(2))
-        ids.append(both(3))
-        group(("gg", t), ids)
-        gres = ["gg%d" % b for b in range(4)]
-        group(("z", t), [
-            act(T.zh[:, 0:128], T.gg[:].indirect(off(O_E, 8)), Act.Copy, gres + ["oe"], ["z0"], scale=0.5),
-            ts(T.zh[:, 128:256], T.gg[:].indirect(off(O_E + 8, 8)), 0.5, None, Alu.mult, None, gres + ["oe"], ["z1"])])
-        quant(T.qz[:], T.pl[:, 640:768], T.zh[:, 0:512], ["z0", "z1", "zero"], ["qz"])
-        ending.append(send(to, T.qz[:, 0:64], T.pl[:, 448:704], lc[:, 0:64], lp[:, 0:256],
-                           T.sem["za%d" % t], T.sem["zl%d" % t], ["qz", "e2", "e3"]))
+        scan(T.ses[:], T.cw8[:], T.se[:], 0.0, Alu.mult, Alu.add, ["cw8", "se"], ["ses"])
+        ts(T.ms[:, M_E:M_E + 8], T.ses[:, 7:K:8], col(C_M8), col(C_A8), Alu.mult, Alu.add, ["ses", "cm8", "ca8"], ["oe"])
+        ending.append(send(to, [[(T.ms[:, 8:16], ml[:, 8:16])]], "e%d" % t, ["oe"]))
 
+        for b in range(4):
+            act(T.fh[:, PL * b:PL * b + C], T["f%d" % b][:, 0:C], Act.Copy, ["psf%d" % b], ["fh%d" % b], scale=0.5)
         act(T.rr[:], T.i64[:].indirect(off(O_R, 4)), Act.Copy, ["i64", "or"], ["rr"])
         if t == 0:
-            zero_landing(0)
             ts(col(C_I1), col(C_I), 1.0, None, Alu.add, None, ["ci"], ["ci1"])
             ts(col(C_M16), col(C_I), 15.0, 1.0 / BIG, Alu.is_equal, Alu.max, ["ci"], ["cm16"])
             ts(T.ca[:], T.tm16[:], col(C_I), None, Alu.not_equal, None, ["tm16", "ci"], ["ca"])
             ts(T.cb[:], T.tm16[:], col(C_I1), BIG, Alu.is_equal, Alu.mult, ["tm16", "ci1"], ["cb"])
             ts(col(C_M16K), col(C_M16), 8.0, None, Alu.mult, None, ["cm16"], ["cm16k"])
             tt(T.cw16[:], T.ca[:], T.cb[:], Alu.max, ["ca", "cb"], ["cw16"])
-        scan(T.ks[:], T.cw16[:], T.kk[:], 0.0, ["cw16", "kk"], ["ks"])
-        ts(off(O_K, 12), T.ks[:, 15:C:16], col(C_M16K), 0.1, Alu.mult, Alu.add, ["ks", "cm16k"], ["ok"])
-        cp(T.cr[:], T.rr[:].indirect(off(O_K, 12)), ["rr", "ok"], ["cr"])
-        if t == ROUNDS - 1:
-            ids = [dma("s", T.ol[gi:gi + 1, :], T.cr[16 * gi:16 * gi + 1, :], ["cr"], ()) for gi in range(8)]
-            group("ol", ids)
-            ending.extend(ids)
-
-        wb = ["pa", "pb", "x0", "x1"]
-        hoist("v", (), ["qh", "h1", "h3"])
-        hoist("a", (), ["h0", "h2"])
-        hoist("p", ["qw", "sw", "lz%d" % t], ["ps" + b for b in wb])
-        arrival(frm, T.sem["za%d" % t], ["lza%d" % t])
-        for b in range(4):
-            mm(wb[b], 128, T.qw[:, 128 * b:128 * b + 128], T.sw[:, 128 * b:128 * b + 128], lc[:, 0:128], lp[:, 192:320],
-               ["qw", "sw", "lza%d" % t, "lz%d" % t])
+        else:
+            scan(T.ks[:], T.cw16[:], T.kk[:], 0.0, Alu.mult, Alu.add, ["cw16", "kk"], ["ks"])
+        arrival(frm, "m%d" % t, 1, ["lm%d" % t])
         ids = []
         for b in range(4):
-            o, i = T.zh[:, 768 + b:1024:4], T[wb[b]][:, 0:K]
+            win, res = T.fh[:, PL * b:PL * b + PL], ["fh%d" % b, "fz%d" % b, "lm%d" % t]
+            a = T.aa[:, K * b:K * b + K]
+            act(a, win.indirect(ml[:, M_F:M_F + 4]), Act.Copy, res, ["fa%d" % b])
+            ids.append(tt(T.gg[:, K * slot[b]:K * slot[b] + K], win.indirect(ml[:, M_S:M_S + 4]), a, Alu.add,
+                          res + ["fa%d" % b], ["gg%d" % b]))
+        group(("gg", t), ids)
+        gres = ["gg%d" % b for b in range(4)]
+
+        wb = ["pa", "pb", "x0", "x1"]
+        hoist("v", gres, ["z1", "qz"])
+        hoist("a", gres, ["z0"])
+        hoist("p", ["qw", "sw"], ["ps" + b for b in wb])
+        arrival(frm, "e%d" % t, 1, ["le%d" % t])
+        group(("z", t), [
+            act(T.zh[:, 0:256:2], T.gg[:, 0:128].indirect(ml[:, M_E:M_E + 8]), Act.Copy, gres + ["le%d" % t], ["z0"]),
+            cp(T.zh[:, 1:256:2], T.gg[:, 128:256].indirect(ml[:, M_E:M_E + 8]), gres + ["le%d" % t], ["z1"])])
+        quant(T.qz[:], T.sz[:], T.zh[:, 0:512], ["z0", "z1", "zero"], ["qz"])
+        for b in range(4):
+            mm(wb[b], 128, T.qw[:, 128 * b:128 * b + 128], T.sw[:, 128 * b:128 * b + 128], T.qz[:], T.sz[:], ["qw", "sw", "qz"])
+        for b in range(4):
+            mm("f%d" % b, C, eq(b)[0], eq(b)[1], T.qt[:], T.st[:], ["e%d" % b, "qt"])
+        if t == 0:
+            scan(T.ks[:], T.cw16[:], T.kk[:], 0.0, Alu.mult, Alu.add, ["cw16", "kk"], ["ks"])
+        ts(off(O_K, 12), T.ks[:, 15:C:16], col(C_M16K), 0.1, Alu.mult, Alu.add, ["ks", "cm16k"], ["ok"])
+        hoist("v", (), ["qh", "h1", "h3"])
+        hoist("a", (), ["h0", "h2"])
+        ids = []
+        for b in range(4):
+            o, i = T.zh[:, 512 + b:768:4], T[wb[b]][:, 0:K]
             if b % 2 == 0:
                 ids.append(act(o, i, Act.Relu, ["ps" + wb[b]], ["h%d" % b], scale=0.03125))
             else:
                 ids.append(ts(o, i, 0.0, 0.03125, Alu.max, Alu.mult, ["ps" + wb[b]], ["h%d" % b]))
         group(("h", t), ids)
-        quant(T.qh[:], T.pl[:, 0:128], T.zh[:, 512:1024], ["h0", "h1", "h2", "h3", "zero"], ["qh"])
-        ending.append(send(frm, T.qh[:, 64:128], T.pl[:, 64:320], lc[:, 192:256], lp[:, 384:640],
-                           T.sem["ha%d" % t], T.sem["hl%d" % t], ["qh", "e0", "e1"]))
+        quant(T.qh[:], T.pl[:, 0:128], T.zh[:, 256:768], ["h0", "h1", "h2", "h3", "zero"], ["qh"])
+        ending.append(send(frm, [[(u8(T.qh[:, K:2 * K]), u8(lc[:, C:C + K])), (T.pl[:, K:5 * K], lp[:, C:C + 4 * K])]],
+                           "h%d" % t, ["qh", "e0", "e1"]))
 
-        scan(T.cs[:], T.cw16[:], T.cr[:], 0.0, ["cw16", "cr"], ["cs"])
+        cp(T.cr[:], T.rr[:].indirect(off(O_K, 12)), ["rr", "ok"], ["cr"])
+        for b in (0, 1):
+            act(T.fb[:, C * b:C * b + C], T["f%d" % b][:, 0:C], Act.Copy, ["psf%d" % b], ["ff%d" % b])
+        scan(T.cs[:], T.cw16[:], T.cr[:], 0.0, Alu.mult, Alu.add, ["cw16", "cr"], ["cs"])
         ts(off(O_C, 12), T.cs[:, 15:C:16], col(C_M16), 0.1, Alu.mult, Alu.add, ["cs", "cm16"], ["oc"])
+        if t == 0:
+            dma("s", T.vt[:], T.v[:], ["qh"], ["vt"])
         if t < ROUNDS - 1:
-            zero_landing(t + 1)
-            prekeys()
+            pre_rows()
+            pre_keys()
         else:
+            ids = [dma("s", T.ol[gi:gi + 1, :], T.cr[16 * gi:16 * gi + 1, :], ["cr"], ()) for gi in range(8)]
+            group("ol", ids)
+            ending.extend(ids)
             quant(T.qv[:], T.sv[:], T.vt[:], ["vt"], ["qv"])
 
         db = ["x0", "x1", "pa", "pb"]
-        hoist("v", (), ["qz", "z1", "qt", "dh0"] + tplanes)
-        hoist("a", ["oc"], ["z0", "dh1", "dh2", "dh3", "tmp2", "tmp3"])
+        hoist("v", ["ff0", "ff1"], ["qt", "dh0", "dh1"] + tplanes)
+        hoist("a", ["oc"], ["dh2", "dh3", "tmp2", "tmp3"])
         hoist("p", (), ["ps" + b for b in db])
-        arrival(to, T.sem["ha%d" % t], ["lha%d" % t])
-        for b in range(4):
-            mm(db[b], 128, eq(b)[0], eq(b)[1], lc[:, 128:256], lp[:, 320:448], ["e%d" % b, "lha%d" % t, "lz%d" % t])
+        arrival(to, "h%d" % t, 1, ["lh%d" % t])
+        for b in (0, 2, 3, 1):
+            mm(db[b], 128, eq(b)[0], eq(b)[1], lc[:, 128:256], lp[:, 128:256], ["e%d" % b, "lh%d" % t, "lt%d" % t])
 
         def dwin(b):
             return T.dh[:, K * b:K * b + K]
 
+        def both(b):
+            return tt(T.tt[:, b:4 * C:4], dwin(b).indirect(off(O_C, 12)), T.fb[:, C * b:C * b + C], Alu.add,
+                      ["dh%d" % b, "oc", "ff%d" % b], [tplanes[b]])
+
+        def plus(b):
+            return tt(T.tt[:, b:4 * C:4], T["f%d" % b][:, 0:C], T.tmp[:, C * (b - 2):C * (b - 1)], Alu.add,
+                      ["psf%d" % b, "tmp%d" % b], [tplanes[b]])
+
         cp(dwin(0), T[db[0]][:, K:2 * K], ["ps" + db[0]], ["dh0"])
-        act(dwin(1), T[db[1]][:, K:2 * K], Act.Copy, ["ps" + db[1]], ["dh1"])
         for b in (2, 3):
             act(dwin(b), T[db[b]][:, K:2 * K], Act.Copy, ["ps" + db[b]], ["dh%d" % b])
             act(T.tmp[:, C * (b - 2):C * (b - 1)], dwin(b).indirect(off(O_C, 12)), Act.Copy, ["dh%d" % b, "oc"], ["tmp%d" % b])
-        ids = [tt(T.tt[:, b:4 * C:4], dwin(b).indirect(off(O_C, 12)), T.fb[:, PL * b:PL * b + C], Alu.add,
-                  ["dh%d" % b, "oc", "ff%d0" % b], [tplanes[b]]) for b in (0, 1)]
-        ids += [tt(T.tt[:, b:4 * C:4], T["f%d" % b][:, 0:C], T.tmp[:, C * (b - 2):C * (b - 1)], Alu.add,
-                   ["psf%d" % b, "tmp%d" % b], [tplanes[b]]) for b in (2, 3)]
+        ids = [both(0)]
+        ids.append(cp(dwin(1), T[db[1]][:, K:2 * K], ["ps" + db[1]], ["dh1"]))
+        ids.pop()
+        ids += [plus(2), both(1), plus(3)]
         group(("t", t), ids)
 
     quant(T.qt[:], T.st[:], T.tt[:], tplanes, ["qt"])
     mm("x0", C, T.qv[:], T.sv[:], T.qt[:], T.st[:], ["qv", "qt"])
-    ending.append(dma("s", T.oc[:], T.qt[:].bitcast(dt.uint8), ["qt"], ()))
+    ending.append(dma("s", T.oc[:], u8(T.qt[:]), ["qt"], ()))
     ids = [dma("a", T.osc[4 * k:4 * k + 4, :], T.st[32 * k:32 * k + 4, :], ["qt"], ()) for k in range(4)]
     group("osc", ids)
     ending.extend(ids)

@@ -3,10 +3,15 @@ from concourse.mybir import dt, AluOpType, ActivationFunctionType
 
 C, K, ROUNDS = 192, 64, 3
 STEP = [1, 2, 3]
-PL = C + K
+AG = C + 1
+NONE = 2 * AG
+PL = 528
 PS = 200
 BIG = 4096.0
-FAR = 256.0
+FAR = 1024.0
+ACTD = 1
+FUSED = 2
+SLOTS = (1, 2, 1)
 
 X4 = "float8_e4m3fn_x4"
 SCRATCH = {
@@ -17,27 +22,28 @@ SCRATCH = {
     "qp": ("sbuf", [128, 256], X4), "sp": ("sbuf", [128, 256], "uint8"),
     "qv": ("sbuf", [128, 128], X4), "sv": ("sbuf", [128, 128], "uint8"),
     "qt": ("sbuf", [128, 192], X4), "st": ("sbuf", [128, 192], "uint8"),
-    "qe": ("sbuf", [128, 512], X4), "pl": ("sbuf", [128, 640], "uint8"),
-    "qz": ("sbuf", [128, 128], X4), "sz": ("sbuf", [128, 128], "uint8"), "qh": ("sbuf", [128, 128], X4),
+    "qe": ("sbuf", [128, 512], X4), "pe": ("sbuf", [128, 512], "uint8"),
+    "qz": ("sbuf", [128, 128], X4), "sz": ("sbuf", [128, 128], "uint8"),
+    "qh": ("sbuf", [128, 128], X4), "sh": ("sbuf", [128, 128], "uint8"),
     "eb": ("sbuf", [128, 520], "bfloat16"), "zh": ("sbuf", [128, 768], "bfloat16"),
-    "ij": ("sbuf", [128, 128], "float32"), "pi": ("sbuf", [128, 8], "int32"), "col": ("sbuf", [128, 16], "float32"),
+    "pi": ("sbuf", [128, 8], "int32"), "col": ("sbuf", [128, 16], "float32"),
     "m16": ("sbuf", [128, 4], "float32"), "kap": ("sbuf", [128, 4], "float32"), "kab": ("sbuf", [128, 4], "float32"),
     "uli": ("sbuf", [128, 16], "int32"),
     "taba": ("sbuf", [128, 64], "bfloat16"), "tabb": ("sbuf", [128, 64], "bfloat16"), "i64": ("sbuf", [128, 64], "bfloat16"),
     "iw": ("sbuf", [128, PL], "float32"), "jr": ("sbuf", [128, C], "bfloat16"),
-    "tm8": ("sbuf", [128, 64], "bfloat16"), "tm16": ("sbuf", [128, 192], "bfloat16"),
+    "tm16": ("sbuf", [128, 192], "bfloat16"),
     "ca": ("sbuf", [128, 192], "bfloat16"), "cb": ("sbuf", [128, 192], "bfloat16"),
     "cc": ("sbuf", [128, 64], "bfloat16"), "cd": ("sbuf", [128, 64], "bfloat16"),
     "cw8": ("sbuf", [128, 64], "bfloat16"), "cw16": ("sbuf", [128, 192], "bfloat16"),
-    "off": ("sbuf", [128, 64], "uint16"), "ms": ("sbuf", [128, 16], "uint16"),
-    "fh": ("sbuf", [128, 4 * PL], "bfloat16"), "fb": ("sbuf", [128, 2 * C], "bfloat16"),
+    "off": ("sbuf", [128, 64], "uint16"), "ms": ("sbuf", [128, 24], "uint16"), "fr": ("sbuf", [128, K], "float32"),
+    "fh": ("sbuf", [128, 4 * PL], "bfloat16"), "fb": ("sbuf", [128, 3 * C], "bfloat16"),
     "aa": ("sbuf", [128, 256], "bfloat16"), "gg": ("sbuf", [128, 256], "float32"),
-    "dh": ("sbuf", [128, 256], "bfloat16"), "tmp": ("sbuf", [128, 384], "bfloat16"),
+    "dh": ("sbuf", [128, 256], "bfloat16"), "tmp": ("sbuf", [128, C], "bfloat16"),
     "ar": ("sbuf", [128, 192], "bfloat16"), "br": ("sbuf", [128, 192], "bfloat16"), "p8": ("sbuf", [128, 192], "bfloat16"),
     "t1": ("sbuf", [128, 192], "bfloat16"), "t2": ("sbuf", [128, 192], "bfloat16"), "sb": ("sbuf", [128, 192], "bfloat16"),
     "kk": ("sbuf", [128, 192], "bfloat16"), "d0": ("sbuf", [128, 768], "bfloat16"),
     "p1": ("sbuf", [128, 4 * PS], "bfloat16"), "p2": ("sbuf", [128, 4 * C], "bfloat16"),
-    "tl": ("sbuf", [128, 4], "float32"), "rk": ("sbuf", [128, 4], "float32"), "junk": ("sbuf", [128, 256], "bfloat16"),
+    "rk": ("sbuf", [128, 4], "float32"), "junk": ("sbuf", [128, 256], "bfloat16"),
     "se": ("sbuf", [128, 64], "bfloat16"), "ses": ("sbuf", [128, 64], "float32"),
     "rr": ("sbuf", [128, 64], "bfloat16"), "ks": ("sbuf", [128, 192], "float32"),
     "cr": ("sbuf", [128, 192], "float32"), "cs": ("sbuf", [128, 192], "float32"),
@@ -45,18 +51,18 @@ SCRATCH = {
 }
 for _t in range(ROUNDS):
     SCRATCH["lc%d" % _t] = ("sbuf", [128, C + K], X4)
-    SCRATCH["lp%d" % _t] = ("sbuf", [128, C + 4 * K], "uint8")
-    SCRATCH["ml%d" % _t] = ("sbuf", [128, 16], "uint16")
+    SCRATCH["lp%d" % _t] = ("sbuf", [128, C + K], "uint8")
+    SCRATCH["ml%d" % _t] = ("sbuf", [128, 24], "uint16")
 for _b in ("pa", "pb", "f0", "f1", "f2", "f3", "x0", "x1"):
     SCRATCH[_b] = ("psum", [128, 512], "float32")
 
 NPOOL, NDMA = 60, 16
-KINDS = ("t", "m", "e", "h")
+KINDS = ("t", "f", "s", "e", "h")
 SEMAPHORES = (["c%d" % k for k in range(NPOOL)] + ["d%d" % k for k in range(NDMA)]
               + ["%s%s%d" % (k, s, t) for k in KINDS for s in "al" for t in range(ROUNDS)])
 
-O_R, O_K, O_C, O_NX, O_U = 0, 4, 16, 28, 40
-M_F, M_S, M_E = 0, 4, 8
+O_R, O_K, O_C, O_NX, O_U, O_F = 0, 4, 16, 28, 40, 56
+M_F, M_S, M_E = 0, 8, 16
 C_I, C_I1, C_Q, C_Q1, C_M8, C_A8, C_M16, C_M16K = 0, 1, 2, 3, 4, 5, 6, 7
 
 
@@ -191,35 +197,36 @@ def rank_program(g, core, T, topo):
     def col(k):
         return T.col[:, k:k + 1]
 
-    def send(to, calls, name, r):
+    def send(to, pairs, name, r, apart=False):
         dst = T.cores[to]
         rid, pid = topo.addr(dst)[:2]
         eng = topo.engines(core, dst)
         rsem, lsem = T.sem[name[0] + "a" + name[1:]], T.sem[name[0] + "l" + name[1:]]
 
         def fn():
-            for pairs in calls:
-                n = len(eng) // len(pairs)
+            for j, (s, d) in enumerate(pairs):
+                mine = eng[j::len(pairs)] if apart else eng
                 g.remote_dma_fused([RemoteDMATransfer(dst_ids=[DstId(rid=rid, pnc=pid)], remote_sem=rsem, src=s, dst=d,
-                                                      dma_engine_mask=sum(1 << e for e in eng[n * k:n * k + n]))
-                                    for k, (s, d) in enumerate(pairs)], local_sem=lsem)
-        return op("g", fn, r, (), kind="remote", sem=(lsem, len(eng) * len(calls)))
+                                                      dma_engine_mask=sum(1 << e for e in mine))], local_sem=lsem)
+        ending.append(op("g", fn, r, (), kind="remote", sem=(lsem, len(eng) * (1 if apart else len(pairs)))))
 
-    def arrival(frm, name, ncalls, w):
-        n = len(topo.engines(T.cores[frm], core)) * ncalls
+    def arrival(frm, name, times, w):
+        n = len(topo.engines(T.cores[frm], core)) * times
         return op(None, None, (), w, kind="arrival", sem=(T.sem[name[0] + "a" + name[1:]], n))
 
     def u8(v):
         return v.bitcast(dt.uint8)
 
     def eq(b):
-        return T.qe[:, 128 * b:128 * b + 128], T.pl[:, 128 + 128 * b:256 + 128 * b]
+        return T.qe[:, 128 * b:128 * b + 128], T.pe[:, 128 * b:128 * b + 128]
 
     def quant_e(b):
         quant(eq(b)[0], eq(b)[1], T.eb[:, 3 - b:515 - b], ["eb"], ["e%d" % b])
 
-    def pre_rows():
+    def odd_row():
         act(T.br[:], T.tabb[:].indirect(off(O_C, 12)), Act.Copy, ["tabb", "oc"], ["br"], scale=0.125)
+
+    def own_row():
         act(T.ar[:], T.taba[:].indirect(off(O_C, 12)), Act.Copy, ["taba", "oc"], ["ar"], scale=0.25)
 
     def pre_keys():
@@ -228,51 +235,50 @@ def rank_program(g, core, T, topo):
     tplanes = ["t0", "t1p", "t2p", "t3"]
     ending = []
 
+    def state(t):
+        quant(T.qt[:], T.st[:], T.tt[:], tplanes, ["qt"])
+        send((rank + STEP[t]) % N, [(u8(T.qt[:]), u8(T["lc%d" % t][:, 0:C])), (T.st[:], T["lp%d" % t][:, 0:C])], "t%d" % t, ["qt"])
+
     dma("a", T.coi[:], T.co[:], (), ["coi"])
     lu = dma("s", T.ut[:], T.u[:], (), ["ut"])
-    lx = dma("a", T.tt[:], T.x[:], (), tplanes)
-    dma("s", T.nxi[:], T.nx[:], (), ["nxi"])
+    dma("a", T.nxi[:], T.nx[:], (), ["nxi"])
+    lx = dma("s", T.tt[:], T.x[:], (), tplanes)
     dma("s", u8(T.qw[:]), T.wc[:], (), ["qw"], after=[lu, lx])
     dma("s", T.sw[:], T.ws[:], (), ["sw"])
 
+    fill(T.eb[:], 0.0, ["eb"])
     iota(T.pi[:, 0:1], [[0, 1]], 0, 1, ["pi0"], small=False)
     iota(T.uli[:], [[1, 2], [16, 8]], 0, 0, ["uli"], small=False)
     iota(T.tabb[:], [[0, 32], [1, 2]], 8, 0, ["tabb"])
     iota(T.taba[:], [[0, 8], [1, 8]], 0, 0, ["taba"])
-    iota(T.ij[:], [[1, 128]], 0, -1, ["ij"])
     iota(T.m16[:], [[16, 4]], 0, 0, ["m16"])
-    iota(T.tm8[:], [[0, 8], [1, 8]], 0, 0, ["tm8"])
-    iota(T.jr[:], [[-1, C]], C - 1, 0, ["jr"])
-    iota(T.iw[:], [[2, PL]], 1, 0, ["iw"])
-    iota(T.i64[:], [[1, 64]], 0, 0, ["i64"])
+    ones = T.eb[:, 3:515:4]
+    op("g", lambda: g.affine_select(ones, ones, [[-1, 128]], Alu.not_equal, 1.0, 0, 1), ["eb"], ["eb"])
+    iota(T.iw[:, 0:PL // 2], [[2, PL // 2]], 1, 0, ["iw0"])
     iota(T.tm16[:], [[0, 12], [1, 16]], 0, 0, ["tm16"])
 
     pini = [T.p1[:, PS * m:PS * m + 1] for m in range(4)]
-    fill(T.eb[:], 0.0, ["eb"])
-    fill(T.zh[:, 256:512], 0.0, ["zero"])
     ts(T.pi[:, 1:2], T.pi[:, 0:1], 15, None, Alu.bitwise_and, None, ["pi0"], ["pi1"])
-    for b in range(4):
-        fill(T.fh[:, PL * b + C:PL * b + PL], 0.0, ["fz%d" % b])
+    fill(T.zh[:, 256:512], 0.0, ["zero"])
+    cp(off(O_U, 16), T.uli[:], ["uli"], ["ou"])
     cp(col(C_I), T.pi[:, 1:2], ["pi1"], ["ci"])
     ts(T.pi[:, 2:3], T.pi[:, 1:2], 1, None, Alu.arith_shift_right, None, ["pi1"], ["pi2"])
     ts(T.pi[:, 3:4], T.pi[:, 1:2], 1, None, Alu.bitwise_and, None, ["pi1"], ["pi3"])
-    cp(off(O_U, 16), T.uli[:], ["uli"], ["ou"])
+    group("fz", [fill(T.fh[:, PL * b + AG + C:PL * b + PL], 0.0, ["fz%d" % b]) for b in range(4)]
+          + [fill(T.fh[:, C:4 * PL:PL], 0.0, ["fz"])])
     cp(col(C_Q), T.pi[:, 2:3], ["pi2"], ["cq"])
     ts(col(C_Q1), T.pi[:, 2:3], 1.0, None, Alu.add, None, ["pi2"], ["cq1"])
+    ts(col(C_M16), col(C_I), 15.0, 1.0 / BIG, Alu.is_equal, Alu.max, ["ci"], ["cm16"])
+    ts(col(C_I1), col(C_I), 1.0, None, Alu.add, None, ["ci"], ["ci1"])
     ts(col(C_A8), T.pi[:, 3:4], float(K), 0.1, Alu.mult, Alu.add, ["pi3"], ["ca8"])
     ts(col(C_M8), T.pi[:, 2:3], 7.0, 1.0 / BIG, Alu.is_equal, Alu.max, ["pi2"], ["cm8"])
-    ts(T.eb[:, 3:515:4], T.ij[:], 0.0, None, Alu.is_equal, None, ["ij"], ["eb"])
-    ts(T.kap[:], T.m16[:], col(C_I), 0.125, Alu.add, Alu.mult, ["m16", "ci"], ["kap"])
-    ts(T.kab[:], T.m16[:], col(C_I), -FAR, Alu.add, Alu.mult, ["m16", "ci"], ["kab"])
-    ts(T.p1[:, 0:4 * PS:PS], T.m16[:], col(C_I), float(C), Alu.add, Alu.add, ["m16", "ci"], ["ini"])
-    quant_e(0)
-    quant_e(1)
     cp(off(O_C, 12), T.coi[:], ["coi"], ["oc"])
-    pre_rows()
-    quant_e(2)
-    quant_e(3)
+    odd_row()
+    ts(T.cc[:], T.taba[:], col(C_Q), None, Alu.not_equal, None, ["taba", "cq"], ["cc"])
+    ts(T.cd[:], T.taba[:], col(C_Q1), BIG, Alu.is_equal, Alu.mult, ["taba", "cq1"], ["cd"])
     quant(T.qu[:], T.su[:], T.ut[:], ["ut"], ["qu"])
-    cp(off(O_NX, 12), T.nxi[:], ["nxi"], ["onx"])
+    ts(T.kap[:], T.m16[:], col(C_I), 0.125, Alu.add, Alu.mult, ["m16", "ci"], ["kap"])
+    tt(T.cw8[:], T.cc[:], T.cd[:], Alu.max, ["cc", "cd"], ["cw8"])
 
     def pick(h):
         o = off(O_U + 8 * h, 8)
@@ -281,6 +287,31 @@ def rank_program(g, core, T, topo):
         act(T.sp[:, s], T.su[:].indirect(o), Act.Copy, ["qu", "ou"], ["sp%d" % h])
 
     pick(0)
+    pick(1)
+    own_row()
+    cp(off(O_NX, 12), T.nxi[:], ["nxi"], ["onx"])
+    state(0)
+    quant_e(0)
+    quant_e(1)
+    act(T.kab[:], T.kap[:], Act.Copy, ["kap"], ["kab"], scale=-8.0 * FAR)
+    act(T.p1[:, 0:4 * PS:PS], T.kap[:], Act.Copy, ["kap"], ["ini"], scale=16.0, bias=float(NONE))
+    act(T.jr[:], T.iw[:, 0:C], Act.Copy, ["iw0"], ["jr"], scale=-0.5, bias=C - 0.5)
+    pre_keys()
+
+    later = [
+        [lambda: quant_e(2)],
+        [lambda: act(T.iw[:, PL // 2:PL], T.iw[:, 0:PL // 2], Act.Copy, ["iw0"], ["iw"], bias=float(PL)),
+         lambda: act(T.i64[:], T.iw[:, 0:K], Act.Copy, ["iw0"], ["i64"], scale=0.5, bias=-0.5)],
+        [lambda: quant_e(3)],
+        [lambda: ts(T.ca[:], T.tm16[:], col(C_I), None, Alu.not_equal, None, ["tm16", "ci"], ["ca"]),
+         lambda: ts(T.cb[:], T.tm16[:], col(C_I1), BIG, Alu.is_equal, Alu.mult, ["tm16", "ci1"], ["cb"])],
+        [lambda: tt(T.cw16[:], T.ca[:], T.cb[:], Alu.max, ["ca", "cb"], ["cw16"])],
+        [lambda: ts(col(C_M16K), col(C_M16), 8.0, None, Alu.mult, None, ["cm16"], ["cm16k"])],
+    ]
+
+    def spare():
+        for fn in (later.pop(0) if later else []):
+            fn()
 
     first = [T.p1[:, PS * m + C:PS * m + C + 1] for m in range(4)]
     second = [T.p2[:, C * m + C - 1:C * m + C] for m in range(4)]
@@ -290,70 +321,116 @@ def rank_program(g, core, T, topo):
     for t in range(ROUNDS):
         to, frm = (rank + STEP[t]) % N, (rank - STEP[t]) % N
         lc, lp, ml = T["lc%d" % t], T["lp%d" % t], T["ml%d" % t]
-        quant(T.qt[:], T.st[:], T.tt[:], tplanes, ["qt"])
-        ending.append(send(to, [[(u8(T.qt[:]), u8(lc[:, 0:C]))], [(T.st[:], lp[:, 0:C])]], "t%d" % t, ["qt"]))
+        if t > 0:
+            state(t)
         mm("pa", C, T.qp[:, 0:128], T.sp[:, 0:128], T.qt[:], T.st[:], ["qp0", "sp0", "qt"])
-        if t == 0:
-            pick(1)
-            pre_keys()
         mm("pb", C, T.qp[:, 128:256], T.sp[:, 128:256], T.qt[:], T.st[:], ["qp1", "sp1", "qt"])
-        arrival(frm, "t%d" % t, 2, ["lt%d" % t])
-        for b in range(4):
-            mm("f%d" % b, C, eq(b)[0], eq(b)[1], lc[:, 0:C], lp[:, 0:C], ["e%d" % b, "lt%d" % t])
-        ts(T.t1[:], T.pa[:, 0:C], 0.0, 4.0, Alu.is_lt, Alu.mult, ["pspa"], ["k1"])
-        act(T.sb[:], T.pb[:, 0:C], Act.Sign, ["pspb"], ["sb"], bias=2.0 ** -120)
-        tt(T.t2[:], T.t1[:], T.p8[:], Alu.add, ["k1", "p8"], ["k2"])
-        tt(T.kk[:], T.t2[:], T.sb[:], Alu.subtract, ["k2", "sb"], ["kk"])
+        halves = [slice(0, C // 2), slice(C // 2, C)]
+        for h, s in enumerate(halves):
+            ts(T.t1[:, s], T.pa[:, s], 0.0, 4.0, Alu.is_lt, Alu.mult, ["pspa"], ["k1%d" % h])
+        for h, s in enumerate(halves):
+            act(T.sb[:, s], T.pb[:, s], Act.Sign, ["pspb"], ["sb%d" % h], bias=2.0 ** -120)
+            tt(T.t2[:, s], T.t1[:, s], T.p8[:, s], Alu.add, ["k1%d" % h, "p8"], ["k2%d" % h])
+        group(("kk", t), [tt(T.kk[:, s], T.t2[:, s], T.sb[:, s], Alu.subtract, ["k2%d" % h, "sb%d" % h], ["kk%d" % h])
+                          for h, s in enumerate(halves)])
+        kres = ["kk%d" % h for h in range(len(halves))]
+        spare()
 
         def dm(m):
             return T.d0[:, C * m:C * m + C]
 
-        act(dm(3), T.kk[:, ::-1], Act.Abs, ["kk", "kab"], ["d03"], scale=8.0 * FAR, bias=T.kab[:, 3:4])
-        for m in range(3):
-            ts(dm(m), T.kk[:, ::-1], T.kap[:, m:m + 1], FAR, Alu.not_equal, Alu.mult, ["kk", "kap"], ["d0%d" % m])
+        for m in range(4 - ACTD, 4):
+            act(dm(m), T.kk[:, ::-1], Act.Abs, kres + ["kab"], ["d0%d" % m], scale=8.0 * FAR, bias=T.kab[:, m:m + 1])
+        for m in range(4 - ACTD):
+            ts(dm(m), T.kk[:, ::-1], T.kap[:, m:m + 1], FAR, Alu.not_equal, Alu.mult, kres + ["kap"], ["d0%d" % m])
+        spare()
         group(("p1", t), [scan(T.p1[:, PS * m + 1:PS * m + 1 + C], dm(m), T.jr[:], pini[m], Alu.min, Alu.max,
                                ["d0%d" % m, "jr", "ini"], [fres[m]]) for m in range(4)])
-        ts(T.ms[:, M_F:M_F + 4], T.p1[:, C:4 * PS:PS], 0.1, None, Alu.add, None, fres, ["of"])
-        group(("rk", t), [act(T.junk[:, K * m:K * m + K], T.iw[:].indirect(T.ms[:, M_F:M_F + 4]), Act.Sign, ["iw", "of", fres[m]],
-                              ["rk%d" % m], scale=-0.5, bias=first[m], accum_out=T.rk[:, m:m + 1]) for m in range(4)])
-        group(("p2", t), [scan(T.p2[:, C * m:C * m + C], dm(m), T.p1[:, PS * m:PS * m + C], pini[m], Alu.min, Alu.max,
-                               ["d0%d" % m, fres[m], "ini"], [sres[m]]) for m in range(4)])
-        if t == 0:
-            ts(T.cc[:], T.tm8[:], col(C_Q), None, Alu.not_equal, None, ["tm8", "cq"], ["cc"])
-            ts(T.cd[:], T.tm8[:], col(C_Q1), BIG, Alu.is_equal, Alu.mult, ["tm8", "cq1"], ["cd"])
-        ts(T.tl[:], T.p2[:, C - 1:4 * C:C], C - 0.5, 4 * FAR, Alu.is_lt, Alu.mult, sres, ["tl"])
-        if t == 0:
-            tt(T.cw8[:], T.cc[:], T.cd[:], Alu.max, ["cc", "cd"], ["cw8"])
-        group(("os", t), [ts(T.ms[:, M_S + m:M_S + m + 1], T.tl[:, m:m + 1], first[m], second[m], Alu.add, Alu.min,
-                             ["tl", fres[m], sres[m]], ["os%d" % m]) for m in range(4)])
-        ending.append(send(to, [[(T.ms[:, 0:8], ml[:, 0:8])]], "m%d" % t, ["of"] + ["os%d" % m for m in range(4)]))
-        ts(off(O_R, 4), T.rk[:], 0.5, 32.1, Alu.mult, Alu.add, ["rk%d" % m for m in range(4)], ["or"])
-        cp(T.se[:].indirect(off(O_R, 4)), T.i64[:], ["or", "i64"], ["se"])
-        scan(T.ses[:], T.cw8[:], T.se[:], 0.0, Alu.mult, Alu.add, ["cw8", "se"], ["ses"])
-        ts(T.ms[:, M_E:M_E + 8], T.ses[:, 7:K:8], col(C_M8), col(C_A8), Alu.mult, Alu.add, ["ses", "cm8", "ca8"], ["oe"])
-        ending.append(send(to, [[(T.ms[:, 8:16], ml[:, 8:16])]], "e%d" % t, ["oe"]))
+        spare()
+        of = off(O_F, 4)
+        ts(of, T.p1[:, C:4 * PS:PS], 0.1, None, Alu.add, None, fres, ["of"])
 
-        for b in range(4):
+        def next_member(m):
+            return scan(T.p2[:, C * m:C * m + C], dm(m), T.p1[:, PS * m:PS * m + C], pini[m], Alu.min, Alu.max,
+                        ["d0%d" % m, fres[m], "ini"], [sres[m]])
+
+        def count(m, row, res):
+            return act(T.junk[:, K * m:K * m + K], row, Act.Sign, res + [fres[m]], ["rk%d" % m], scale=-0.5, bias=first[m],
+                       accum_out=T.rk[:, m:m + 1])
+
+        ts(T.ms[:, M_F:M_F + 4], T.p1[:, C:4 * PS:PS], float(C), None, Alu.min, None, fres, ["om"])
+        send(to, [(T.ms[:, M_F:M_F + 4], ml[:, M_F:M_F + 4])], "f%d" % t, ["om"])
+        next_member(0)
+        if FUSED < 4:
+            cp(T.fr[:], T.iw[:].indirect(of), ["iw", "of"], ["fr"])
+        for m in (1, 2, 3):
+            next_member(m)
+        group(("rk", t), [count(m, T.iw[:].indirect(of), ["iw", "of"]) for m in range(FUSED)]
+              + [count(m, T.fr[:], ["fr"]) for m in range(FUSED, 4)])
+        group(("os", t), [ts(T.ms[:, M_S + m:M_S + m + 1], first[m], float(AG), second[m], Alu.add, Alu.min,
+                             [fres[m], sres[m]], ["os%d" % m]) for m in range(4)])
+        send(to, [(T.ms[:, M_S:M_S + 4], ml[:, M_S:M_S + 4])], "s%d" % t, ["os%d" % m for m in range(4)])
+
+        def unpack():
+            arrival(frm, "t%d" % t, 2, ["lt%d" % t])
+            for b in range(4):
+                mm("f%d" % b, C, eq(b)[0], eq(b)[1], lc[:, 0:C], lp[:, 0:C], ["e%d" % b, "lt%d" % t])
+
+        def halved(b):
             act(T.fh[:, PL * b:PL * b + C], T["f%d" % b][:, 0:C], Act.Copy, ["psf%d" % b], ["fh%d" % b], scale=0.5)
-        act(T.rr[:], T.i64[:].indirect(off(O_R, 4)), Act.Copy, ["i64", "or"], ["rr"])
+
+        def again(b):
+            cp(T.fh[:, PL * b + AG:PL * b + AG + C], T.fh[:, PL * b:PL * b + C], ["fh%d" % b], ["fg%d" % b])
+
+        def firsts(b):
+            act(T.aa[:, K * b:K * b + K], T.fh[:, PL * b:PL * b + AG].indirect(ml[:, M_F:M_F + 4]), Act.Copy,
+                ["fh%d" % b, "fz", "lf%d" % t], ["fa%d" % b])
+
+        def seconds(b):
+            return tt(T.gg[:, K * slot[b]:K * slot[b] + K], T.fh[:, PL * b:PL * b + PL].indirect(ml[:, M_S:M_S + 4]),
+                      T.aa[:, K * b:K * b + K], Alu.add, ["fh%d" % b, "fg%d" % b, "fz", "fa%d" % b, "ls%d" % t], ["gg%d" % b])
+
+        def key_row():
+            scan(T.ks[:], T.cw16[:], T.kk[:], 0.0, Alu.mult, Alu.add, ["cw16"] + kres, ["ks"])
+
+        def key_list():
+            ts(off(O_K, 12), T.ks[:, 15:C:16], col(C_M16K), 0.1, Alu.mult, Alu.add, ["ks", "cm16k"], ["ok"])
+
+        side = [key_row, key_list] + [lambda b=b: again(b) for b in range(4)]
+        slots = list(SLOTS)
+        unpack()
+        if t > 0:
+            for b in range(4):
+                halved(b)
+
+        def between():
+            if t > 0:
+                for k in range(slots.pop(0)):
+                    side.pop(0)()
+            spare()
+
+        ts(off(O_R, 4), T.rk[:], 0.5, 32.1, Alu.mult, Alu.add, ["rk%d" % m for m in range(4)], ["or"])
+        between()
+        cp(T.se[:].indirect(off(O_R, 4)), T.i64[:], ["or", "i64"], ["se"])
+        between()
+        scan(T.ses[:], T.cw8[:], T.se[:], 0.0, Alu.mult, Alu.add, ["cw8", "se"], ["ses"])
+        between()
+        ts(T.ms[:, M_E:M_E + 8], T.ses[:, 7:K:8], col(C_M8), col(C_A8), Alu.mult, Alu.add, ["ses", "cm8", "ca8"], ["oe"])
+        send(to, [(T.ms[:, M_E:M_E + 8], ml[:, M_E:M_E + 8])], "e%d" % t, ["oe"])
+
+        arrival(frm, "f%d" % t, 1, ["lf%d" % t])
+        arrival(frm, "s%d" % t, 1, ["ls%d" % t])
         if t == 0:
-            ts(col(C_I1), col(C_I), 1.0, None, Alu.add, None, ["ci"], ["ci1"])
-            ts(col(C_M16), col(C_I), 15.0, 1.0 / BIG, Alu.is_equal, Alu.max, ["ci"], ["cm16"])
-            ts(T.ca[:], T.tm16[:], col(C_I), None, Alu.not_equal, None, ["tm16", "ci"], ["ca"])
-            ts(T.cb[:], T.tm16[:], col(C_I1), BIG, Alu.is_equal, Alu.mult, ["tm16", "ci1"], ["cb"])
-            ts(col(C_M16K), col(C_M16), 8.0, None, Alu.mult, None, ["cm16"], ["cm16k"])
-            tt(T.cw16[:], T.ca[:], T.cb[:], Alu.max, ["ca", "cb"], ["cw16"])
+            side.insert(3, side.pop(1))
+            for step, b in ((halved, 0), (halved, 1), (firsts, 0), (halved, 2), (firsts, 1), (halved, 3), (firsts, 2), (firsts, 3)):
+                step(b)
         else:
-            scan(T.ks[:], T.cw16[:], T.kk[:], 0.0, Alu.mult, Alu.add, ["cw16", "kk"], ["ks"])
-        arrival(frm, "m%d" % t, 1, ["lm%d" % t])
-        ids = []
-        for b in range(4):
-            win, res = T.fh[:, PL * b:PL * b + PL], ["fh%d" % b, "fz%d" % b, "lm%d" % t]
-            a = T.aa[:, K * b:K * b + K]
-            act(a, win.indirect(ml[:, M_F:M_F + 4]), Act.Copy, res, ["fa%d" % b])
-            ids.append(tt(T.gg[:, K * slot[b]:K * slot[b] + K], win.indirect(ml[:, M_S:M_S + 4]), a, Alu.add,
-                          res + ["fa%d" % b], ["gg%d" % b]))
-        group(("gg", t), ids)
+            for b in range(4):
+                firsts(b)
+        for fn in side:
+            fn()
+        group(("gg", t), [seconds(b) for b in range(4)])
+        act(T.rr[:], T.i64[:].indirect(off(O_R, 4)), Act.Copy, ["i64", "or"], ["rr"])
         gres = ["gg%d" % b for b in range(4)]
 
         wb = ["pa", "pb", "x0", "x1"]
@@ -369,45 +446,41 @@ def rank_program(g, core, T, topo):
             mm(wb[b], 128, T.qw[:, 128 * b:128 * b + 128], T.sw[:, 128 * b:128 * b + 128], T.qz[:], T.sz[:], ["qw", "sw", "qz"])
         for b in range(4):
             mm("f%d" % b, C, eq(b)[0], eq(b)[1], T.qt[:], T.st[:], ["e%d" % b, "qt"])
-        if t == 0:
-            scan(T.ks[:], T.cw16[:], T.kk[:], 0.0, Alu.mult, Alu.add, ["cw16", "kk"], ["ks"])
-        ts(off(O_K, 12), T.ks[:, 15:C:16], col(C_M16K), 0.1, Alu.mult, Alu.add, ["ks", "cm16k"], ["ok"])
-        hoist("v", (), ["qh", "h1", "h3"])
-        hoist("a", (), ["h0", "h2"])
+
+        cp(T.cr[:], T.rr[:].indirect(off(O_K, 12)), ["rr", "ok"], ["cr"])
+        scan(T.cs[:], T.cw16[:], T.cr[:], 0.0, Alu.mult, Alu.add, ["cw16", "cr"], ["cs"])
+        ts(off(O_C, 12), T.cs[:, 15:C:16], col(C_M16), 0.1, Alu.mult, Alu.add, ["cs", "cm16"], ["oc"])
+        hoist("v", (), ["qh", "h3"])
+        hoist("a", (), ["h0", "h1", "h2"])
         ids = []
         for b in range(4):
             o, i = T.zh[:, 512 + b:768:4], T[wb[b]][:, 0:K]
-            if b % 2 == 0:
+            if b < 3:
                 ids.append(act(o, i, Act.Relu, ["ps" + wb[b]], ["h%d" % b], scale=0.03125))
             else:
                 ids.append(ts(o, i, 0.0, 0.03125, Alu.max, Alu.mult, ["ps" + wb[b]], ["h%d" % b]))
         group(("h", t), ids)
-        quant(T.qh[:], T.pl[:, 0:128], T.zh[:, 256:768], ["h0", "h1", "h2", "h3", "zero"], ["qh"])
-        ending.append(send(frm, [[(u8(T.qh[:, K:2 * K]), u8(lc[:, C:C + K])), (T.pl[:, K:5 * K], lp[:, C:C + 4 * K])]],
-                           "h%d" % t, ["qh", "e0", "e1"]))
+        quant(T.qh[:], T.sh[:], T.zh[:, 256:768], ["h0", "h1", "h2", "h3", "zero"], ["qh"])
+        send(frm, [(u8(T.qh[:, K:2 * K]), u8(lc[:, C:C + K])), (T.sh[:, K:2 * K], lp[:, C:C + K])], "h%d" % t, ["qh"], apart=True)
 
-        cp(T.cr[:], T.rr[:].indirect(off(O_K, 12)), ["rr", "ok"], ["cr"])
-        for b in (0, 1):
-            act(T.fb[:, C * b:C * b + C], T["f%d" % b][:, 0:C], Act.Copy, ["psf%d" % b], ["ff%d" % b])
-        scan(T.cs[:], T.cw16[:], T.cr[:], 0.0, Alu.mult, Alu.add, ["cw16", "cr"], ["cs"])
-        ts(off(O_C, 12), T.cs[:, 15:C:16], col(C_M16), 0.1, Alu.mult, Alu.add, ["cs", "cm16"], ["oc"])
-        if t == 0:
-            dma("s", T.vt[:], T.v[:], ["qh"], ["vt"])
         if t < ROUNDS - 1:
-            pre_rows()
+            odd_row()
+            own_row()
             pre_keys()
         else:
-            ids = [dma("s", T.ol[gi:gi + 1, :], T.cr[16 * gi:16 * gi + 1, :], ["cr"], ()) for gi in range(8)]
-            group("ol", ids)
-            ending.extend(ids)
+            ending.append(dma("s", T.ol[:], T.cr[0:128:16, :], ["cr"], ()))
             quant(T.qv[:], T.sv[:], T.vt[:], ["vt"], ["qv"])
+        for b in range(3):
+            act(T.fb[:, C * b:C * b + C], T["f%d" % b][:, 0:C], Act.Copy, ["psf%d" % b], ["ff%d" % b])
 
         db = ["x0", "x1", "pa", "pb"]
-        hoist("v", ["ff0", "ff1"], ["qt", "dh0", "dh1"] + tplanes)
-        hoist("a", ["oc"], ["dh2", "dh3", "tmp2", "tmp3"])
+        hoist("v", ["ff0", "ff1", "ff2"], ["qt", "dh0"] + tplanes)
+        hoist("a", ["oc"], ["dh1", "dh2", "dh3", "tmp"])
         hoist("p", (), ["ps" + b for b in db])
         arrival(to, "h%d" % t, 1, ["lh%d" % t])
-        for b in (0, 2, 3, 1):
+        if t == 0:
+            dma("s", T.vt[:], T.v[:], ["lh0"], ["vt"])
+        for b in (0, 1, 3, 2):
             mm(db[b], 128, eq(b)[0], eq(b)[1], lc[:, 128:256], lp[:, 128:256], ["e%d" % b, "lh%d" % t, "lt%d" % t])
 
         def dwin(b):
@@ -417,24 +490,17 @@ def rank_program(g, core, T, topo):
             return tt(T.tt[:, b:4 * C:4], dwin(b).indirect(off(O_C, 12)), T.fb[:, C * b:C * b + C], Alu.add,
                       ["dh%d" % b, "oc", "ff%d" % b], [tplanes[b]])
 
-        def plus(b):
-            return tt(T.tt[:, b:4 * C:4], T["f%d" % b][:, 0:C], T.tmp[:, C * (b - 2):C * (b - 1)], Alu.add,
-                      ["psf%d" % b, "tmp%d" % b], [tplanes[b]])
-
         cp(dwin(0), T[db[0]][:, K:2 * K], ["ps" + db[0]], ["dh0"])
-        for b in (2, 3):
+        for b in (1, 3, 2):
             act(dwin(b), T[db[b]][:, K:2 * K], Act.Copy, ["ps" + db[b]], ["dh%d" % b])
-            act(T.tmp[:, C * (b - 2):C * (b - 1)], dwin(b).indirect(off(O_C, 12)), Act.Copy, ["dh%d" % b, "oc"], ["tmp%d" % b])
-        ids = [both(0)]
-        ids.append(cp(dwin(1), T[db[1]][:, K:2 * K], ["ps" + db[1]], ["dh1"]))
-        ids.pop()
-        ids += [plus(2), both(1), plus(3)]
-        group(("t", t), ids)
+        act(T.tmp[:], dwin(3).indirect(off(O_C, 12)), Act.Copy, ["dh3", "oc"], ["tmp"])
+        group(("t", t), [both(0), both(1), both(2),
+                         tt(T.tt[:, 3:4 * C:4], T.f3[:, 0:C], T.tmp[:], Alu.add, ["psf3", "tmp"], [tplanes[3]])])
 
     quant(T.qt[:], T.st[:], T.tt[:], tplanes, ["qt"])
     mm("x0", C, T.qv[:], T.sv[:], T.qt[:], T.st[:], ["qv", "qt"])
-    ending.append(dma("s", T.oc[:], u8(T.qt[:]), ["qt"], ()))
-    ids = [dma("a", T.osc[4 * k:4 * k + 4, :], T.st[32 * k:32 * k + 4, :], ["qt"], ()) for k in range(4)]
+    ending.append(dma("a", T.oc[:], u8(T.qt[:]), ["qt"], ()))
+    ids = [dma("sa"[k // 2], T.osc[4 * k:4 * k + 4, :], T.st[32 * k:32 * k + 4, :], ["qt"], ()) for k in range(4)]
     group("osc", ids)
     ending.extend(ids)
     cp(T.yo[:], T.x0[:, 0:C], ["psx0"], ["yo"])

@@ -1,17 +1,14 @@
-from concourse.bass import DstId, RemoteDMATransfer
 from concourse.mybir import dt, AluOpType, ActivationFunctionType
 
 C, K, ROUNDS = 192, 64, 3
 STEP = [1, 2, 3]
-AG = C + 1
-NONE = 2 * AG
-PL = 528
+PL = C + K
 PS = 200
 BIG = 4096.0
 FAR = 1024.0
-ACTD = 1
+ACTD = 2
 FUSED = 2
-SLOTS = (1, 2, 1)
+ORDER = "n0 of n1 fr n2 n3 ks tl or os se ok ses"
 
 X4 = "float8_e4m3fn_x4"
 SCRATCH = {
@@ -26,8 +23,8 @@ SCRATCH = {
     "qz": ("sbuf", [128, 128], X4), "sz": ("sbuf", [128, 128], "uint8"),
     "qh": ("sbuf", [128, 128], X4), "sh": ("sbuf", [128, 128], "uint8"),
     "eb": ("sbuf", [128, 520], "bfloat16"), "zh": ("sbuf", [128, 768], "bfloat16"),
-    "pi": ("sbuf", [128, 8], "int32"), "col": ("sbuf", [128, 16], "float32"),
-    "m16": ("sbuf", [128, 4], "float32"), "kap": ("sbuf", [128, 4], "float32"), "kab": ("sbuf", [128, 4], "float32"),
+    "pi": ("sbuf", [128, 8], "int32"), "col": ("sbuf", [128, 8], "float32"), "colb": ("sbuf", [128, 4], "bfloat16"),
+    "m16": ("sbuf", [128, 4], "float32"), "kap": ("sbuf", [128, 4], "bfloat16"), "kab": ("sbuf", [128, 4], "float32"),
     "uli": ("sbuf", [128, 16], "int32"),
     "taba": ("sbuf", [128, 64], "bfloat16"), "tabb": ("sbuf", [128, 64], "bfloat16"), "i64": ("sbuf", [128, 64], "bfloat16"),
     "iw": ("sbuf", [128, PL], "float32"), "jr": ("sbuf", [128, C], "bfloat16"),
@@ -43,7 +40,7 @@ SCRATCH = {
     "t1": ("sbuf", [128, 192], "bfloat16"), "t2": ("sbuf", [128, 192], "bfloat16"), "sb": ("sbuf", [128, 192], "bfloat16"),
     "kk": ("sbuf", [128, 192], "bfloat16"), "d0": ("sbuf", [128, 768], "bfloat16"),
     "p1": ("sbuf", [128, 4 * PS], "bfloat16"), "p2": ("sbuf", [128, 4 * C], "bfloat16"),
-    "rk": ("sbuf", [128, 4], "float32"), "junk": ("sbuf", [128, 256], "bfloat16"),
+    "tl": ("sbuf", [128, 4], "float32"), "rk": ("sbuf", [128, 4], "float32"), "junk": ("sbuf", [128, 256], "bfloat16"),
     "se": ("sbuf", [128, 64], "bfloat16"), "ses": ("sbuf", [128, 64], "float32"),
     "rr": ("sbuf", [128, 64], "bfloat16"), "ks": ("sbuf", [128, 192], "float32"),
     "cr": ("sbuf", [128, 192], "float32"), "cs": ("sbuf", [128, 192], "float32"),
@@ -61,7 +58,7 @@ KINDS = ("t", "f", "s", "e", "h")
 SEMAPHORES = (["c%d" % k for k in range(NPOOL)] + ["d%d" % k for k in range(NDMA)]
               + ["%s%s%d" % (k, s, t) for k in KINDS for s in "al" for t in range(ROUNDS)])
 
-O_R, O_K, O_C, O_NX, O_U, O_F = 0, 4, 16, 28, 40, 56
+O_R, O_K, O_C, O_NX, O_U = 0, 4, 16, 28, 40
 M_F, M_S, M_E = 0, 8, 16
 C_I, C_I1, C_Q, C_Q1, C_M8, C_A8, C_M16, C_M16K = 0, 1, 2, 3, 4, 5, 6, 7
 
@@ -195,20 +192,18 @@ def rank_program(g, core, T, topo):
         return T.off[:, o:o + k]
 
     def col(k):
-        return T.col[:, k:k + 1]
+        return (T.colb if k in (C_I, C_I1, C_Q, C_Q1) else T.col)[:, k:k + 1]
 
-    def send(to, pairs, name, r, apart=False):
+    def send(to, pairs, name, r):
         dst = T.cores[to]
         rid, pid = topo.addr(dst)[:2]
         eng = topo.engines(core, dst)
         rsem, lsem = T.sem[name[0] + "a" + name[1:]], T.sem[name[0] + "l" + name[1:]]
 
         def fn():
-            for j, (s, d) in enumerate(pairs):
-                mine = eng[j::len(pairs)] if apart else eng
-                g.remote_dma_fused([RemoteDMATransfer(dst_ids=[DstId(rid=rid, pnc=pid)], remote_sem=rsem, src=s, dst=d,
-                                                      dma_engine_mask=sum(1 << e for e in mine))], local_sem=lsem)
-        ending.append(op("g", fn, r, (), kind="remote", sem=(lsem, len(eng) * (1 if apart else len(pairs)))))
+            for s, d in pairs:
+                g.remote_dma(d, s, rsem, lsem, pid, rid, topo.mask(core, dst))
+        ending.append(op("g", fn, r, (), kind="remote", sem=(lsem, len(eng) * len(pairs))))
 
     def arrival(frm, name, times, w):
         n = len(topo.engines(T.cores[frm], core)) * times
@@ -241,44 +236,47 @@ def rank_program(g, core, T, topo):
 
     dma("a", T.coi[:], T.co[:], (), ["coi"])
     lu = dma("s", T.ut[:], T.u[:], (), ["ut"])
-    dma("a", T.nxi[:], T.nx[:], (), ["nxi"])
-    lx = dma("s", T.tt[:], T.x[:], (), tplanes)
-    dma("s", u8(T.qw[:]), T.wc[:], (), ["qw"], after=[lu, lx])
+    dma("a", T.tt[:], T.x[:], (), tplanes)
+    dma("s", T.nxi[:], T.nx[:], (), ["nxi"])
+    dma("s", u8(T.qw[:]), T.wc[:], (), ["qw"], after=[lu])
     dma("s", T.sw[:], T.ws[:], (), ["sw"])
 
     fill(T.eb[:], 0.0, ["eb"])
     iota(T.pi[:, 0:1], [[0, 1]], 0, 1, ["pi0"], small=False)
-    iota(T.uli[:], [[1, 2], [16, 8]], 0, 0, ["uli"], small=False)
-    iota(T.tabb[:], [[0, 32], [1, 2]], 8, 0, ["tabb"])
-    iota(T.taba[:], [[0, 8], [1, 8]], 0, 0, ["taba"])
     iota(T.m16[:], [[16, 4]], 0, 0, ["m16"])
     ones = T.eb[:, 3:515:4]
     op("g", lambda: g.affine_select(ones, ones, [[-1, 128]], Alu.not_equal, 1.0, 0, 1), ["eb"], ["eb"])
-    iota(T.iw[:, 0:PL // 2], [[2, PL // 2]], 1, 0, ["iw0"])
+    iota(T.taba[:], [[0, 8], [1, 8]], 0, 0, ["taba"])
+    iota(T.uli[:], [[1, 2], [16, 8]], 0, 0, ["uli"], small=False)
+    iota(T.tabb[:], [[0, 32], [1, 2]], 8, 0, ["tabb"])
+    iota(T.iw[:], [[2, PL]], 1, 0, ["iw"])
     iota(T.tm16[:], [[0, 12], [1, 16]], 0, 0, ["tm16"])
 
     pini = [T.p1[:, PS * m:PS * m + 1] for m in range(4)]
-    ts(T.pi[:, 1:2], T.pi[:, 0:1], 15, None, Alu.bitwise_and, None, ["pi0"], ["pi1"])
     fill(T.zh[:, 256:512], 0.0, ["zero"])
-    cp(off(O_U, 16), T.uli[:], ["uli"], ["ou"])
+    ts(T.pi[:, 1:2], T.pi[:, 0:1], 15, None, Alu.bitwise_and, None, ["pi0"], ["pi1"])
+    group("fz", [fill(T.fh[:, PL * b + C:PL * b + PL], 0.0, ["fz%d" % b]) for b in range(4)])
     cp(col(C_I), T.pi[:, 1:2], ["pi1"], ["ci"])
     ts(T.pi[:, 2:3], T.pi[:, 1:2], 1, None, Alu.arith_shift_right, None, ["pi1"], ["pi2"])
     ts(T.pi[:, 3:4], T.pi[:, 1:2], 1, None, Alu.bitwise_and, None, ["pi1"], ["pi3"])
-    group("fz", [fill(T.fh[:, PL * b + AG + C:PL * b + PL], 0.0, ["fz%d" % b]) for b in range(4)]
-          + [fill(T.fh[:, C:4 * PL:PL], 0.0, ["fz"])])
+    ts(col(C_M16), T.pi[:, 1:2], 15.0, 1.0 / BIG, Alu.is_equal, Alu.max, ["pi1"], ["cm16"])
+    ts(col(C_I1), T.pi[:, 1:2], 1.0, None, Alu.add, None, ["pi1"], ["ci1"])
+    ts(T.kap[:], T.m16[:], col(C_I), 0.125, Alu.add, Alu.mult, ["m16", "ci"], ["kap"])
     cp(col(C_Q), T.pi[:, 2:3], ["pi2"], ["cq"])
     ts(col(C_Q1), T.pi[:, 2:3], 1.0, None, Alu.add, None, ["pi2"], ["cq1"])
-    ts(col(C_M16), col(C_I), 15.0, 1.0 / BIG, Alu.is_equal, Alu.max, ["ci"], ["cm16"])
-    ts(col(C_I1), col(C_I), 1.0, None, Alu.add, None, ["ci"], ["ci1"])
-    ts(col(C_A8), T.pi[:, 3:4], float(K), 0.1, Alu.mult, Alu.add, ["pi3"], ["ca8"])
-    ts(col(C_M8), T.pi[:, 2:3], 7.0, 1.0 / BIG, Alu.is_equal, Alu.max, ["pi2"], ["cm8"])
-    cp(off(O_C, 12), T.coi[:], ["coi"], ["oc"])
-    odd_row()
+    act(T.kab[:], T.kap[:], Act.Copy, ["kap"], ["kab"], scale=-8.0 * FAR)
+    act(T.p1[:, 0:4 * PS:PS], T.kap[:], Act.Copy, ["kap"], ["ini"], scale=8.0, bias=float(C))
+    act(col(C_M16K), col(C_M16), Act.Copy, ["cm16"], ["cm16k"], scale=8.0)
+    for b in range(4):
+        quant_e(b)
+    cp(off(O_U, 16), T.uli[:], ["uli"], ["ou"])
     ts(T.cc[:], T.taba[:], col(C_Q), None, Alu.not_equal, None, ["taba", "cq"], ["cc"])
     ts(T.cd[:], T.taba[:], col(C_Q1), BIG, Alu.is_equal, Alu.mult, ["taba", "cq1"], ["cd"])
+    ts(col(C_A8), T.pi[:, 3:4], float(K), 0.1, Alu.mult, Alu.add, ["pi3"], ["ca8"])
+    cp(off(O_C, 12), T.coi[:], ["coi"], ["oc"])
+    own_row()
     quant(T.qu[:], T.su[:], T.ut[:], ["ut"], ["qu"])
-    ts(T.kap[:], T.m16[:], col(C_I), 0.125, Alu.add, Alu.mult, ["m16", "ci"], ["kap"])
-    tt(T.cw8[:], T.cc[:], T.cd[:], Alu.max, ["cc", "cd"], ["cw8"])
+    ts(T.br[:], T.tabb[:].indirect(off(O_C, 12)), 0.125, None, Alu.mult, None, ["tabb", "oc"], ["br"])
 
     def pick(h):
         o = off(O_U + 8 * h, 8)
@@ -287,30 +285,23 @@ def rank_program(g, core, T, topo):
         act(T.sp[:, s], T.su[:].indirect(o), Act.Copy, ["qu", "ou"], ["sp%d" % h])
 
     pick(0)
-    pick(1)
-    own_row()
-    cp(off(O_NX, 12), T.nxi[:], ["nxi"], ["onx"])
     state(0)
-    quant_e(0)
-    quant_e(1)
-    act(T.kab[:], T.kap[:], Act.Copy, ["kap"], ["kab"], scale=-8.0 * FAR)
-    act(T.p1[:, 0:4 * PS:PS], T.kap[:], Act.Copy, ["kap"], ["ini"], scale=16.0, bias=float(NONE))
-    act(T.jr[:], T.iw[:, 0:C], Act.Copy, ["iw0"], ["jr"], scale=-0.5, bias=C - 0.5)
+    cp(off(O_NX, 12), T.nxi[:], ["nxi"], ["onx"])
+    pick(1)
     pre_keys()
 
-    later = [
-        [lambda: quant_e(2)],
-        [lambda: act(T.iw[:, PL // 2:PL], T.iw[:, 0:PL // 2], Act.Copy, ["iw0"], ["iw"], bias=float(PL)),
-         lambda: act(T.i64[:], T.iw[:, 0:K], Act.Copy, ["iw0"], ["i64"], scale=0.5, bias=-0.5)],
-        [lambda: quant_e(3)],
-        [lambda: ts(T.ca[:], T.tm16[:], col(C_I), None, Alu.not_equal, None, ["tm16", "ci"], ["ca"]),
-         lambda: ts(T.cb[:], T.tm16[:], col(C_I1), BIG, Alu.is_equal, Alu.mult, ["tm16", "ci1"], ["cb"])],
-        [lambda: tt(T.cw16[:], T.ca[:], T.cb[:], Alu.max, ["ca", "cb"], ["cw16"])],
-        [lambda: ts(col(C_M16K), col(C_M16), 8.0, None, Alu.mult, None, ["cm16"], ["cm16k"])],
-    ]
+    later = {
+        "t1": [lambda: ts(T.ca[:], T.tm16[:], col(C_I), None, Alu.not_equal, None, ["tm16", "ci"], ["ca"])],
+        "t2": [lambda: ts(T.cb[:], T.tm16[:], col(C_I1), BIG, Alu.is_equal, Alu.mult, ["tm16", "ci1"], ["cb"]),
+               lambda: act(T.jr[:], T.iw[:, 0:C], Act.Copy, ["iw"], ["jr"], scale=-0.5, bias=C - 0.5)],
+        "kk": [lambda: tt(T.cw16[:], T.ca[:], T.cb[:], Alu.max, ["ca", "cb"], ["cw16"])],
+        "d0": [lambda: act(T.i64[:], T.iw[:, 0:K], Act.Copy, ["iw"], ["i64"], scale=0.5, bias=-0.5),
+               lambda: tt(T.cw8[:], T.cc[:], T.cd[:], Alu.max, ["cc", "cd"], ["cw8"])],
+        "se": [lambda: ts(col(C_M8), T.pi[:, 2:3], 7.0, 1.0 / BIG, Alu.is_equal, Alu.max, ["pi2"], ["cm8"])],
+    }
 
-    def spare():
-        for fn in (later.pop(0) if later else []):
+    def spare(behind):
+        for fn in later.pop(behind, []):
             fn()
 
     first = [T.p1[:, PS * m + C:PS * m + C + 1] for m in range(4)]
@@ -325,113 +316,112 @@ def rank_program(g, core, T, topo):
             state(t)
         mm("pa", C, T.qp[:, 0:128], T.sp[:, 0:128], T.qt[:], T.st[:], ["qp0", "sp0", "qt"])
         mm("pb", C, T.qp[:, 128:256], T.sp[:, 128:256], T.qt[:], T.st[:], ["qp1", "sp1", "qt"])
+        if t > 0:
+            hoist("v", ["p8"], ["of", "oe", "se", "ses", "or", "ok", "tl", "fr", "ks", "d00", "d0h", "d01", "kk0", "kk1"]
+                  + ["os%d" % m for m in range(4)] + fres + sres)
+            hoist("a", (), ["sb0", "sb1", "d02", "d03", "rr", "cr"] + ["rk%d" % m for m in range(4)])
         halves = [slice(0, C // 2), slice(C // 2, C)]
         for h, s in enumerate(halves):
             ts(T.t1[:, s], T.pa[:, s], 0.0, 4.0, Alu.is_lt, Alu.mult, ["pspa"], ["k1%d" % h])
+        spare("t1")
         for h, s in enumerate(halves):
             act(T.sb[:, s], T.pb[:, s], Act.Sign, ["pspb"], ["sb%d" % h], bias=2.0 ** -120)
             tt(T.t2[:, s], T.t1[:, s], T.p8[:, s], Alu.add, ["k1%d" % h, "p8"], ["k2%d" % h])
-        group(("kk", t), [tt(T.kk[:, s], T.t2[:, s], T.sb[:, s], Alu.subtract, ["k2%d" % h, "sb%d" % h], ["kk%d" % h])
-                          for h, s in enumerate(halves)])
+        spare("t2")
+        for h, s in enumerate(halves):
+            tt(T.kk[:, s], T.t2[:, s], T.sb[:, s], Alu.subtract, ["k2%d" % h, "sb%d" % h], ["kk%d" % h])
         kres = ["kk%d" % h for h in range(len(halves))]
-        spare()
+        spare("kk")
 
         def dm(m):
             return T.d0[:, C * m:C * m + C]
 
         for m in range(4 - ACTD, 4):
             act(dm(m), T.kk[:, ::-1], Act.Abs, kres + ["kab"], ["d0%d" % m], scale=8.0 * FAR, bias=T.kab[:, m:m + 1])
-        for m in range(4 - ACTD):
+        group(("d0", t), [ts(T.d0[:, C // 2:C], T.kk[:, C // 2 - 1::-1], T.kap[:, 0:1], FAR, Alu.not_equal, Alu.mult, ["kk0", "kap"], ["d0h"]),
+                          ts(T.d0[:, 0:C // 2], T.kk[:, C - 1:C // 2 - 1:-1], T.kap[:, 0:1], FAR, Alu.not_equal, Alu.mult, ["kk1", "kap"], ["d00"])])
+        for m in range(1, 4 - ACTD):
             ts(dm(m), T.kk[:, ::-1], T.kap[:, m:m + 1], FAR, Alu.not_equal, Alu.mult, kres + ["kap"], ["d0%d" % m])
-        spare()
+        dres = [["d00", "d0h"], ["d01"], ["d02"], ["d03"]]
+        spare("d0")
         group(("p1", t), [scan(T.p1[:, PS * m + 1:PS * m + 1 + C], dm(m), T.jr[:], pini[m], Alu.min, Alu.max,
-                               ["d0%d" % m, "jr", "ini"], [fres[m]]) for m in range(4)])
-        spare()
-        of = off(O_F, 4)
-        ts(of, T.p1[:, C:4 * PS:PS], 0.1, None, Alu.add, None, fres, ["of"])
+                               dres[m] + ["jr", "ini"], [fres[m]]) for m in range(4)][1:])
+        of = T.ms[:, M_F:M_F + 4]
 
         def next_member(m):
-            return scan(T.p2[:, C * m:C * m + C], dm(m), T.p1[:, PS * m:PS * m + C], pini[m], Alu.min, Alu.max,
-                        ["d0%d" % m, fres[m], "ini"], [sres[m]])
+            group(("p2", t), [scan(T.p2[:, C * m:C * m + C], dm(m), T.p1[:, PS * m:PS * m + C], pini[m], Alu.min, Alu.max,
+                                   dres[m] + [fres[m], "ini"], [sres[m]])])
 
         def count(m, row, res):
             return act(T.junk[:, K * m:K * m + K], row, Act.Sign, res + [fres[m]], ["rk%d" % m], scale=-0.5, bias=first[m],
                        accum_out=T.rk[:, m:m + 1])
 
-        ts(T.ms[:, M_F:M_F + 4], T.p1[:, C:4 * PS:PS], float(C), None, Alu.min, None, fres, ["om"])
-        send(to, [(T.ms[:, M_F:M_F + 4], ml[:, M_F:M_F + 4])], "f%d" % t, ["om"])
-        next_member(0)
-        if FUSED < 4:
-            cp(T.fr[:], T.iw[:].indirect(of), ["iw", "of"], ["fr"])
-        for m in (1, 2, 3):
-            next_member(m)
-        group(("rk", t), [count(m, T.iw[:].indirect(of), ["iw", "of"]) for m in range(FUSED)]
-              + [count(m, T.fr[:], ["fr"]) for m in range(FUSED, 4)])
-        group(("os", t), [ts(T.ms[:, M_S + m:M_S + m + 1], first[m], float(AG), second[m], Alu.add, Alu.min,
-                             [fres[m], sres[m]], ["os%d" % m]) for m in range(4)])
-        send(to, [(T.ms[:, M_S:M_S + 4], ml[:, M_S:M_S + 4])], "s%d" % t, ["os%d" % m for m in range(4)])
-
-        def unpack():
-            arrival(frm, "t%d" % t, 2, ["lt%d" % t])
-            for b in range(4):
-                mm("f%d" % b, C, eq(b)[0], eq(b)[1], lc[:, 0:C], lp[:, 0:C], ["e%d" % b, "lt%d" % t])
-
         def halved(b):
             act(T.fh[:, PL * b:PL * b + C], T["f%d" % b][:, 0:C], Act.Copy, ["psf%d" % b], ["fh%d" % b], scale=0.5)
 
-        def again(b):
-            cp(T.fh[:, PL * b + AG:PL * b + AG + C], T.fh[:, PL * b:PL * b + C], ["fh%d" % b], ["fg%d" % b])
-
         def firsts(b):
-            act(T.aa[:, K * b:K * b + K], T.fh[:, PL * b:PL * b + AG].indirect(ml[:, M_F:M_F + 4]), Act.Copy,
-                ["fh%d" % b, "fz", "lf%d" % t], ["fa%d" % b])
+            act(T.aa[:, K * b:K * b + K], T.fh[:, PL * b:PL * b + PL].indirect(ml[:, M_F:M_F + 4]), Act.Copy,
+                ["fh%d" % b, "fz%d" % b, "lf%d" % t], ["fa%d" % b])
 
         def seconds(b):
             return tt(T.gg[:, K * slot[b]:K * slot[b] + K], T.fh[:, PL * b:PL * b + PL].indirect(ml[:, M_S:M_S + 4]),
-                      T.aa[:, K * b:K * b + K], Alu.add, ["fh%d" % b, "fg%d" % b, "fz", "fa%d" % b, "ls%d" % t], ["gg%d" % b])
+                      T.aa[:, K * b:K * b + K], Alu.add, ["fh%d" % b, "fz%d" % b, "fa%d" % b, "ls%d" % t], ["gg%d" % b])
 
-        def key_row():
-            scan(T.ks[:], T.cw16[:], T.kk[:], 0.0, Alu.mult, Alu.add, ["cw16"] + kres, ["ks"])
+        def first_list():
+            ts(of, T.p1[:, C:4 * PS:PS], 0.1, None, Alu.add, None, fres, ["of"])
+            send(to, [(of, ml[:, M_F:M_F + 4])], "f%d" % t, ["of"])
 
-        def key_list():
-            ts(off(O_K, 12), T.ks[:, 15:C:16], col(C_M16K), 0.1, Alu.mult, Alu.add, ["ks", "cm16k"], ["ok"])
-
-        side = [key_row, key_list] + [lambda b=b: again(b) for b in range(4)]
-        slots = list(SLOTS)
-        unpack()
-        if t > 0:
-            for b in range(4):
+        def ranks():
+            cp(T.fr[:], T.iw[:].indirect(of), ["iw", "of"], ["fr"])
+            group(("rk", t), [count(m, T.iw[:].indirect(of), ["iw", "of"]) for m in range(FUSED)]
+                  + [count(m, T.fr[:], ["fr"]) for m in range(FUSED, 4)])
+            for b in range(4 if t > 0 else 2):
                 halved(b)
 
-        def between():
-            if t > 0:
-                for k in range(slots.pop(0)):
-                    side.pop(0)()
-            spare()
+        arrival(frm, "t%d" % t, 2, ["lt%d" % t])
+        for b in range(4):
+            mm("f%d" % b, C, eq(b)[0], eq(b)[1], lc[:, 0:C], lp[:, 0:C], ["e%d" % b, "lt%d" % t])
 
-        ts(off(O_R, 4), T.rk[:], 0.5, 32.1, Alu.mult, Alu.add, ["rk%d" % m for m in range(4)], ["or"])
-        between()
-        cp(T.se[:].indirect(off(O_R, 4)), T.i64[:], ["or", "i64"], ["se"])
-        between()
-        scan(T.ses[:], T.cw8[:], T.se[:], 0.0, Alu.mult, Alu.add, ["cw8", "se"], ["ses"])
-        between()
+        def second_list():
+            group(("os", t), [ts(T.ms[:, M_S + m:M_S + m + 1], T.tl[:, m:m + 1], first[m], second[m], Alu.add, Alu.min,
+                                 ["tl", fres[m], sres[m]], ["os%d" % m]) for m in range(4)])
+            send(to, [(T.ms[:, M_S:M_S + 4], ml[:, M_S:M_S + 4])], "s%d" % t, ["os%d" % m for m in range(4)])
+
+        steps = {
+            "of": first_list, "fr": ranks, "os": second_list,
+            "tl": lambda: ts(T.tl[:], T.p2[:, C - 1:4 * C:C], C - 0.5, FAR, Alu.is_lt, Alu.mult, sres, ["tl"]),
+            "or": lambda: ts(off(O_R, 4), T.rk[:], 0.5, 32.1, Alu.mult, Alu.add, ["rk%d" % m for m in range(4)], ["or"]),
+            "se": lambda: cp(T.se[:].indirect(off(O_R, 4)), T.i64[:], ["or", "i64"], ["se"]),
+            "ses": lambda: scan(T.ses[:], T.cw8[:], T.se[:], 0.0, Alu.mult, Alu.add, ["cw8", "se"], ["ses"]),
+            "ks": lambda: scan(T.ks[:], T.cw16[:], T.kk[:], 0.0, Alu.mult, Alu.add, ["cw16"] + kres, ["ks"]),
+            "ok": lambda: ts(off(O_K, 12), T.ks[:, 15:C:16], col(C_M16K), 0.1, Alu.mult, Alu.add, ["ks", "cm16k"], ["ok"]),
+        }
+        for m in range(4):
+            steps["n%d" % m] = lambda m=m: next_member(m)
+        for name in ORDER.split():
+            steps[name]()
+            spare(name)
         ts(T.ms[:, M_E:M_E + 8], T.ses[:, 7:K:8], col(C_M8), col(C_A8), Alu.mult, Alu.add, ["ses", "cm8", "ca8"], ["oe"])
         send(to, [(T.ms[:, M_E:M_E + 8], ml[:, M_E:M_E + 8])], "e%d" % t, ["oe"])
 
         arrival(frm, "f%d" % t, 1, ["lf%d" % t])
         arrival(frm, "s%d" % t, 1, ["ls%d" % t])
         if t == 0:
-            side.insert(3, side.pop(1))
-            for step, b in ((halved, 0), (halved, 1), (firsts, 0), (halved, 2), (firsts, 1), (halved, 3), (firsts, 2), (firsts, 3)):
+            for step, b in ((firsts, 0), (halved, 2), (firsts, 1), (halved, 3), (firsts, 2), (firsts, 3)):
                 step(b)
         else:
             for b in range(4):
                 firsts(b)
-        for fn in side:
-            fn()
         group(("gg", t), [seconds(b) for b in range(4)])
         act(T.rr[:], T.i64[:].indirect(off(O_R, 4)), Act.Copy, ["i64", "or"], ["rr"])
         gres = ["gg%d" % b for b in range(4)]
+
+        def own_f():
+            for b in range(4):
+                mm("f%d" % b, C, eq(b)[0], eq(b)[1], T.qt[:], T.st[:], ["e%d" % b, "qt"])
+
+        if t > 0:
+            own_f()
 
         wb = ["pa", "pb", "x0", "x1"]
         hoist("v", gres, ["z1", "qz"])
@@ -444,10 +434,10 @@ def rank_program(g, core, T, topo):
         quant(T.qz[:], T.sz[:], T.zh[:, 0:512], ["z0", "z1", "zero"], ["qz"])
         for b in range(4):
             mm(wb[b], 128, T.qw[:, 128 * b:128 * b + 128], T.sw[:, 128 * b:128 * b + 128], T.qz[:], T.sz[:], ["qw", "sw", "qz"])
-        for b in range(4):
-            mm("f%d" % b, C, eq(b)[0], eq(b)[1], T.qt[:], T.st[:], ["e%d" % b, "qt"])
+        if t == 0:
+            own_f()
 
-        cp(T.cr[:], T.rr[:].indirect(off(O_K, 12)), ["rr", "ok"], ["cr"])
+        act(T.cr[:], T.rr[:].indirect(off(O_K, 12)), Act.Copy, ["rr", "ok"], ["cr"])
         scan(T.cs[:], T.cw16[:], T.cr[:], 0.0, Alu.mult, Alu.add, ["cw16", "cr"], ["cs"])
         ts(off(O_C, 12), T.cs[:, 15:C:16], col(C_M16), 0.1, Alu.mult, Alu.add, ["cs", "cm16"], ["oc"])
         hoist("v", (), ["qh", "h3"])
@@ -461,7 +451,7 @@ def rank_program(g, core, T, topo):
                 ids.append(ts(o, i, 0.0, 0.03125, Alu.max, Alu.mult, ["ps" + wb[b]], ["h%d" % b]))
         group(("h", t), ids)
         quant(T.qh[:], T.sh[:], T.zh[:, 256:768], ["h0", "h1", "h2", "h3", "zero"], ["qh"])
-        send(frm, [(u8(T.qh[:, K:2 * K]), u8(lc[:, C:C + K])), (T.sh[:, K:2 * K], lp[:, C:C + K])], "h%d" % t, ["qh"], apart=True)
+        send(frm, [(u8(T.qh[:, K:2 * K]), u8(lc[:, C:C + K])), (T.sh[:, K:2 * K], lp[:, C:C + K])], "h%d" % t, ["qh"])
 
         if t < ROUNDS - 1:
             odd_row()
@@ -474,10 +464,10 @@ def rank_program(g, core, T, topo):
             act(T.fb[:, C * b:C * b + C], T["f%d" % b][:, 0:C], Act.Copy, ["psf%d" % b], ["ff%d" % b])
 
         db = ["x0", "x1", "pa", "pb"]
-        hoist("v", ["ff0", "ff1", "ff2"], ["qt", "dh0"] + tplanes)
+        hoist("v", (), ["qt", "dh0"] + tplanes)
         hoist("a", ["oc"], ["dh1", "dh2", "dh3", "tmp"])
         hoist("p", (), ["ps" + b for b in db])
-        arrival(to, "h%d" % t, 1, ["lh%d" % t])
+        arrival(to, "h%d" % t, 2, ["lh%d" % t])
         if t == 0:
             dma("s", T.vt[:], T.v[:], ["lh0"], ["vt"])
         for b in (0, 1, 3, 2):
@@ -491,6 +481,7 @@ def rank_program(g, core, T, topo):
                       ["dh%d" % b, "oc", "ff%d" % b], [tplanes[b]])
 
         cp(dwin(0), T[db[0]][:, K:2 * K], ["ps" + db[0]], ["dh0"])
+        hoist("v", ["ff0", "ff1", "ff2"])
         for b in (1, 3, 2):
             act(dwin(b), T[db[b]][:, K:2 * K], Act.Copy, ["ps" + db[b]], ["dh%d" % b])
         act(T.tmp[:], dwin(3).indirect(off(O_C, 12)), Act.Copy, ["dh3", "oc"], ["tmp"])
@@ -499,11 +490,11 @@ def rank_program(g, core, T, topo):
 
     quant(T.qt[:], T.st[:], T.tt[:], tplanes, ["qt"])
     mm("x0", C, T.qv[:], T.sv[:], T.qt[:], T.st[:], ["qv", "qt"])
-    ending.append(dma("a", T.oc[:], u8(T.qt[:]), ["qt"], ()))
-    ids = [dma("sa"[k // 2], T.osc[4 * k:4 * k + 4, :], T.st[32 * k:32 * k + 4, :], ["qt"], ()) for k in range(4)]
+    ending.append(dma("s", T.oc[:], u8(T.qt[:]), ["qt"], ()))
+    ids = [dma("s", T.osc[4 * k:4 * k + 4, :], T.st[32 * k:32 * k + 4, :], ["qt"], ()) for k in range(4)]
     group("osc", ids)
     ending.extend(ids)
-    cp(T.yo[:], T.x0[:, 0:C], ["psx0"], ["yo"])
-    ending.append(dma("s", T.y[:], T.yo[:], ["yo"], ()))
+    act(T.yo[:], T.x0[:, 0:C], Act.Copy, ["psx0"], ["yo"])
+    ending.append(dma("a", T.y[:], T.yo[:], ["yo"], ()))
     op("g", None, (), (), after=ending)
     emit(g, T, ops)

from concourse.mybir import dt, AluOpType, ActivationFunctionType

C, K, ROUNDS = 192, 64, 3
STEP = [1, 2, 3]
PL = C + K
PS = 200
BIG = 4096.0
FAR = 1024.0
ACTD = 2
FUSED = 2
ORDER = "n0 of n1 fr n2 n3 ks tl or os se ok ses"

X4 = "float8_e4m3fn_x4"
SCRATCH = {
    "tt": ("sbuf", [128, 768], "bfloat16"), "ut": ("sbuf", [128, 512], "bfloat16"), "vt": ("sbuf", [128, 512], "bfloat16"),
    "nxi": ("sbuf", [128, 12], "int32"), "coi": ("sbuf", [128, 12], "int32"),
    "qw": ("sbuf", [128, 512], X4), "sw": ("sbuf", [128, 512], "uint8"),
    "qu": ("sbuf", [128, 128], X4), "su": ("sbuf", [128, 128], "uint8"),
    "qp": ("sbuf", [128, 256], X4), "sp": ("sbuf", [128, 256], "uint8"),
    "qv": ("sbuf", [128, 128], X4), "sv": ("sbuf", [128, 128], "uint8"),
    "qt": ("sbuf", [128, 192], X4), "st": ("sbuf", [128, 192], "uint8"),
    "qe": ("sbuf", [128, 512], X4), "pe": ("sbuf", [128, 512], "uint8"),
    "qz": ("sbuf", [128, 128], X4), "sz": ("sbuf", [128, 128], "uint8"),
    "qh": ("sbuf", [128, 128], X4), "sh": ("sbuf", [128, 128], "uint8"),
    "eb": ("sbuf", [128, 520], "bfloat16"), "zh": ("sbuf", [128, 768], "bfloat16"),
    "pi": ("sbuf", [128, 8], "int32"), "col": ("sbuf", [128, 8], "float32"), "colb": ("sbuf", [128, 4], "bfloat16"),
    "m16": ("sbuf", [128, 4], "float32"), "kap": ("sbuf", [128, 4], "bfloat16"), "kab": ("sbuf", [128, 4], "float32"),
    "uli": ("sbuf", [128, 16], "int32"),
    "taba": ("sbuf", [128, 64], "bfloat16"), "tabb": ("sbuf", [128, 64], "bfloat16"), "i64": ("sbuf", [128, 64], "bfloat16"),
    "iw": ("sbuf", [128, PL], "float32"), "jr": ("sbuf", [128, C], "bfloat16"),
    "tm16": ("sbuf", [128, 192], "bfloat16"),
    "ca": ("sbuf", [128, 192], "bfloat16"), "cb": ("sbuf", [128, 192], "bfloat16"),
    "cc": ("sbuf", [128, 64], "bfloat16"), "cd": ("sbuf", [128, 64], "bfloat16"),
    "cw8": ("sbuf", [128, 64], "bfloat16"), "cw16": ("sbuf", [128, 192], "bfloat16"),
    "off": ("sbuf", [128, 64], "uint16"), "ms": ("sbuf", [128, 24], "uint16"), "fr": ("sbuf", [128, K], "float32"),
    "fh": ("sbuf", [128, 4 * PL], "bfloat16"), "fb": ("sbuf", [128, 3 * C], "bfloat16"),
    "aa": ("sbuf", [128, 256], "bfloat16"), "gg": ("sbuf", [128, 256], "float32"),
    "dh": ("sbuf", [128, 256], "bfloat16"), "tmp": ("sbuf", [128, C], "bfloat16"),
    "ar": ("sbuf", [128, 192], "bfloat16"), "br": ("sbuf", [128, 192], "bfloat16"), "p8": ("sbuf", [128, 192], "bfloat16"),
    "t1": ("sbuf", [128, 192], "bfloat16"), "t2": ("sbuf", [128, 192], "bfloat16"), "sb": ("sbuf", [128, 192], "bfloat16"),
    "kk": ("sbuf", [128, 192], "bfloat16"), "d0": ("sbuf", [128, 768], "bfloat16"),
    "p1": ("sbuf", [128, 4 * PS], "bfloat16"), "p2": ("sbuf", [128, 4 * C], "bfloat16"),
    "tl": ("sbuf", [128, 4], "float32"), "rk": ("sbuf", [128, 4], "float32"), "junk": ("sbuf", [128, 256], "bfloat16"),
    "se": ("sbuf", [128, 64], "bfloat16"), "ses": ("sbuf", [128, 64], "float32"),
    "rr": ("sbuf", [128, 64], "bfloat16"), "ks": ("sbuf", [128, 192], "float32"),
    "cr": ("sbuf", [128, 192], "float32"), "cs": ("sbuf", [128, 192], "float32"),
    "yo": ("sbuf", [128, 192], "float32"),
}
for _t in range(ROUNDS):
    SCRATCH["lc%d" % _t] = ("sbuf", [128, C + K], X4)
    SCRATCH["lp%d" % _t] = ("sbuf", [128, C + K], "uint8")
    SCRATCH["ml%d" % _t] = ("sbuf", [128, 24], "uint16")
for _b in ("pa", "pb", "f0", "f1", "f2", "f3", "x0", "x1"):
    SCRATCH[_b] = ("psum", [128, 512], "float32")

NPOOL, NDMA = 60, 16
KINDS = ("t", "f", "s", "e", "h")
SEMAPHORES = (["c%d" % k for k in range(NPOOL)] + ["d%d" % k for k in range(NDMA)]
              + ["%s%s%d" % (k, s, t) for k in KINDS for s in "al" for t in range(ROUNDS)])

O_R, O_K, O_C, O_NX, O_U = 0, 4, 16, 28, 40
M_F, M_S, M_E = 0, 8, 16
C_I, C_I1, C_Q, C_Q1, C_M8, C_A8, C_M16, C_M16K = 0, 1, 2, 3, 4, 5, 6, 7


def emit(g, T, ops):
    queue = {"g": g, "v": g.vector, "a": g.scalar, "p": g.tensor, "s": g.sync}
    last_w, readers, known, members = {}, {}, {q: set() for q in queue}, {}
    for n, o in enumerate(ops):
        if o["grp"] is None:
            o["grp"] = ("own", n)
        members.setdefault(o["grp"], []).append(n)
    for n, o in enumerate(ops):
        deps = set(o["after"])
        for r in o["r"]:
            if r in last_w:
                deps.add(last_w[r])
            if r.startswith("ps"):
                deps.update(k for k in readers.get(r, []) if ops[k]["q"] != o["q"])
        for w in o["w"]:
            if w in last_w:
                deps.add(last_w[w])
            deps.update(readers.get(w, []))
        deps.discard(n)
        if o["kind"] != "hoist":
            for r in o["r"]:
                readers.setdefault(r, []).append(n)
            for w in o["w"]:
                last_w[w] = n
                readers[w] = []
        if o["q"] is None:
            o["know"], o["waits"] = set(), []
            continue
        kn = known[o["q"]]
        deps = sorted(d for d in deps if d not in kn)
        deps = [d for d in deps if not any(d in ops[e]["know"] for e in deps if e != d)]
        o["waits"] = []
        for d in deps:
            if d in kn:
                continue
            o["waits"].append(d)
            for e in members[ops[d]["grp"]]:
                assert e < n
                ops[e]["needed"] = True
                kn.add(e)
                kn.update(ops[e]["know"])
        o["know"] = set(kn)
    user, count, ndma, given = [[] for k in range(NPOOL)], [0] * NPOOL, [0], {}
    for n, o in enumerate(ops):
        if o["q"] is None:
            continue
        q = queue[o["q"]]
        for d in o["waits"]:
            q.wait_ge(ops[d]["sem"][0], ops[d]["sem"][1])
        if o["fn"] is None:
            continue
        ins = o["fn"]()
        if o["kind"] == "dma":
            if o["grp"] not in given:
                given[o["grp"]] = (T.sem["d%d" % ndma[0]], 16 * len(members[o["grp"]]))
                ndma[0] += 1
            o["sem"] = given[o["grp"]]
            ins.then_inc(o["sem"][0], 16)
        elif o["kind"] == "op" and o["needed"]:
            if o["grp"] not in given:
                mem = members[o["grp"]]
                k = [j for j in range(NPOOL) if all(u in ops[e]["know"] for u in user[j] for e in mem)][0]
                user[k] = mem
                count[k] += len(mem)
                given[o["grp"]] = (T.sem["c%d" % k], count[k])
            o["sem"] = given[o["grp"]]
            ins.then_inc(o["sem"][0], 1)


def rank_program(g, core, T, topo):
    rank = T.rank_of(core)
    if rank is None:
        return
    N = len(T.cores)
    V, A, P = g.vector, g.scalar, g.tensor
    Alu, Act = AluOpType, ActivationFunctionType
    ops = []

    def op(q, fn, r=(), w=(), after=(), kind="op", sem=None):
        ops.append({"q": q, "fn": fn, "r": list(r), "w": list(w), "after": list(after), "kind": kind, "sem": sem,
                    "needed": False, "grp": None})
        return len(ops) - 1

    def group(name, ids):
        for k in ids:
            ops[k]["grp"] = name

    def hoist(q, r=(), w=()):
        op(q, None, r, w, kind="hoist")

    def dma(q, out, in_, r=(), w=(), after=()):
        e = {"s": g.sync, "a": g.scalar}[q]
        return op(q, lambda: e.dma_start(out, in_), r, w, after, kind="dma")

    def ts(out, in0, s1, s2, o0, o1, r, w):
        if o1 is None:
            return op("v", lambda: V.tensor_scalar(out, in0, s1, None, o0), r, w)
        return op("v", lambda: V.tensor_scalar(out, in0, s1, s2, o0, o1), r, w)

    def tt(out, a, b, o, r, w):
        return op("v", lambda: V.tensor_tensor(out, a, b, o), r, w)

    def cp(out, in_, r, w):
        return op("v", lambda: V.tensor_copy(out, in_), r, w)

    def act(out, in_, f, r, w, **kw):
        return op("a", lambda: A.activation(out, in_, f, **kw), r, w)

    def quant(q, s, x, r, w):
        return op("v", lambda: V.quantize_mx(q, s, x), r, w)

    def mm(bank, n, lq, ls, rq, rs, r):
        return op("p", lambda: P.matmul_mx(T[bank][:, 0:n], lq, ls, rq, rs, True, True), r, ["ps" + bank])

    def scan(out, d0, d1, init, o0, o1, r, w):
        return op("v", lambda: V.tensor_tensor_scan(out, d0, d1, init, o0, o1), r, w)

    def iota(out, pat, base, cm, w, small=True):
        if small:
            return op("g", lambda: g.iota(out, pat, base, cm, allow_small_or_imprecise_dtypes=True), (), w)
        return op("g", lambda: g.iota(out, pat, base, cm), (), w)

    def fill(ap, c, w):
        return op("v", lambda: V.memset(ap, c), (), w)

    def off(o, k):
        return T.off[:, o:o + k]

    def col(k):
        return (T.colb if k in (C_I, C_I1, C_Q, C_Q1) else T.col)[:, k:k + 1]

    def send(to, pairs, name, r):
        dst = T.cores[to]
        rid, pid = topo.addr(dst)[:2]
        eng = topo.engines(core, dst)
        rsem, lsem = T.sem[name[0] + "a" + name[1:]], T.sem[name[0] + "l" + name[1:]]

        def fn():
            for s, d in pairs:
                g.remote_dma(d, s, rsem, lsem, pid, rid, topo.mask(core, dst))
        ending.append(op("g", fn, r, (), kind="remote", sem=(lsem, len(eng) * len(pairs))))

    def arrival(frm, name, times, w):
        n = len(topo.engines(T.cores[frm], core)) * times
        return op(None, None, (), w, kind="arrival", sem=(T.sem[name[0] + "a" + name[1:]], n))

    def u8(v):
        return v.bitcast(dt.uint8)

    def eq(b):
        return T.qe[:, 128 * b:128 * b + 128], T.pe[:, 128 * b:128 * b + 128]

    def quant_e(b):
        quant(eq(b)[0], eq(b)[1], T.eb[:, 3 - b:515 - b], ["eb"], ["e%d" % b])

    def odd_row():
        act(T.br[:], T.tabb[:].indirect(off(O_C, 12)), Act.Copy, ["tabb", "oc"], ["br"], scale=0.125)

    def own_row():
        act(T.ar[:], T.taba[:].indirect(off(O_C, 12)), Act.Copy, ["taba", "oc"], ["ar"], scale=0.25)

    def pre_keys():
        tt(T.p8[:], T.br[:].indirect(off(O_NX, 12)), T.ar[:], Alu.add, ["br", "ar", "onx"], ["p8"])

    tplanes = ["t0", "t1p", "t2p", "t3"]
    ending = []

    def state(t):
        quant(T.qt[:], T.st[:], T.tt[:], tplanes, ["qt"])
        send((rank + STEP[t]) % N, [(u8(T.qt[:]), u8(T["lc%d" % t][:, 0:C])), (T.st[:], T["lp%d" % t][:, 0:C])], "t%d" % t, ["qt"])

    dma("a", T.coi[:], T.co[:], (), ["coi"])
    lu = dma("s", T.ut[:], T.u[:], (), ["ut"])
    dma("a", T.tt[:], T.x[:], (), tplanes)
    dma("s", T.nxi[:], T.nx[:], (), ["nxi"])
    dma("s", u8(T.qw[:]), T.wc[:], (), ["qw"], after=[lu])
    dma("s", T.sw[:], T.ws[:], (), ["sw"])

    fill(T.eb[:], 0.0, ["eb"])
    iota(T.pi[:, 0:1], [[0, 1]], 0, 1, ["pi0"], small=False)
    iota(T.m16[:], [[16, 4]], 0, 0, ["m16"])
    ones = T.eb[:, 3:515:4]
    op("g", lambda: g.affine_select(ones, ones, [[-1, 128]], Alu.not_equal, 1.0, 0, 1), ["eb"], ["eb"])
    iota(T.taba[:], [[0, 8], [1, 8]], 0, 0, ["taba"])
    iota(T.uli[:], [[1, 2], [16, 8]], 0, 0, ["uli"], small=False)
    iota(T.tabb[:], [[0, 32], [1, 2]], 8, 0, ["tabb"])
    iota(T.iw[:], [[2, PL]], 1, 0, ["iw"])
    iota(T.tm16[:], [[0, 12], [1, 16]], 0, 0, ["tm16"])

    pini = [T.p1[:, PS * m:PS * m + 1] for m in range(4)]
    fill(T.zh[:, 256:512], 0.0, ["zero"])
    ts(T.pi[:, 1:2], T.pi[:, 0:1], 15, None, Alu.bitwise_and, None, ["pi0"], ["pi1"])
    group("fz", [fill(T.fh[:, PL * b + C:PL * b + PL], 0.0, ["fz%d" % b]) for b in range(4)])
    cp(col(C_I), T.pi[:, 1:2], ["pi1"], ["ci"])
    ts(T.pi[:, 2:3], T.pi[:, 1:2], 1, None, Alu.arith_shift_right, None, ["pi1"], ["pi2"])
    ts(T.pi[:, 3:4], T.pi[:, 1:2], 1, None, Alu.bitwise_and, None, ["pi1"], ["pi3"])
    ts(col(C_M16), T.pi[:, 1:2], 15.0, 1.0 / BIG, Alu.is_equal, Alu.max, ["pi1"], ["cm16"])
    ts(col(C_I1), T.pi[:, 1:2], 1.0, None, Alu.add, None, ["pi1"], ["ci1"])
    ts(T.kap[:], T.m16[:], col(C_I), 0.125, Alu.add, Alu.mult, ["m16", "ci"], ["kap"])
    cp(col(C_Q), T.pi[:, 2:3], ["pi2"], ["cq"])
    ts(col(C_Q1), T.pi[:, 2:3], 1.0, None, Alu.add, None, ["pi2"], ["cq1"])
    act(T.kab[:], T.kap[:], Act.Copy, ["kap"], ["kab"], scale=-8.0 * FAR)
    act(T.p1[:, 0:4 * PS:PS], T.kap[:], Act.Copy, ["kap"], ["ini"], scale=8.0, bias=float(C))
    act(col(C_M16K), col(C_M16), Act.Copy, ["cm16"], ["cm16k"], scale=8.0)
    for b in range(4):
        quant_e(b)
    cp(off(O_U, 16), T.uli[:], ["uli"], ["ou"])
    ts(T.cc[:], T.taba[:], col(C_Q), None, Alu.not_equal, None, ["taba", "cq"], ["cc"])
    ts(T.cd[:], T.taba[:], col(C_Q1), BIG, Alu.is_equal, Alu.mult, ["taba", "cq1"], ["cd"])
    ts(col(C_A8), T.pi[:, 3:4], float(K), 0.1, Alu.mult, Alu.add, ["pi3"], ["ca8"])
    cp(off(O_C, 12), T.coi[:], ["coi"], ["oc"])
    own_row()
    quant(T.qu[:], T.su[:], T.ut[:], ["ut"], ["qu"])
    ts(T.br[:], T.tabb[:].indirect(off(O_C, 12)), 0.125, None, Alu.mult, None, ["tabb", "oc"], ["br"])

    def pick(h):
        o = off(O_U + 8 * h, 8)
        s = slice(128 * h, 128 * h + 128)
        op("v", lambda: V.tensor_copy(T.qp[:, s].bitcast(dt.uint32), T.qu[:].bitcast(dt.uint32).indirect(o)), ["qu", "ou"], ["qp%d" % h])
        act(T.sp[:, s], T.su[:].indirect(o), Act.Copy, ["qu", "ou"], ["sp%d" % h])

    pick(0)
    state(0)
    cp(off(O_NX, 12), T.nxi[:], ["nxi"], ["onx"])
    pick(1)
    pre_keys()

    later = {
        "t1": [lambda: ts(T.ca[:], T.tm16[:], col(C_I), None, Alu.not_equal, None, ["tm16", "ci"], ["ca"])],
        "t2": [lambda: ts(T.cb[:], T.tm16[:], col(C_I1), BIG, Alu.is_equal, Alu.mult, ["tm16", "ci1"], ["cb"]),
               lambda: act(T.jr[:], T.iw[:, 0:C], Act.Copy, ["iw"], ["jr"], scale=-0.5, bias=C - 0.5)],
        "kk": [lambda: tt(T.cw16[:], T.ca[:], T.cb[:], Alu.max, ["ca", "cb"], ["cw16"])],
        "d0": [lambda: act(T.i64[:], T.iw[:, 0:K], Act.Copy, ["iw"], ["i64"], scale=0.5, bias=-0.5),
               lambda: tt(T.cw8[:], T.cc[:], T.cd[:], Alu.max, ["cc", "cd"], ["cw8"])],
        "se": [lambda: ts(col(C_M8), T.pi[:, 2:3], 7.0, 1.0 / BIG, Alu.is_equal, Alu.max, ["pi2"], ["cm8"])],
    }

    def spare(behind):
        for fn in later.pop(behind, []):
            fn()

    first = [T.p1[:, PS * m + C:PS * m + C + 1] for m in range(4)]
    second = [T.p2[:, C * m + C - 1:C * m + C] for m in range(4)]
    fres, sres = ["p1%d" % m for m in range(4)], ["p2%d" % m for m in range(4)]
    slot = [0, 2, 1, 3]

    for t in range(ROUNDS):
        to, frm = (rank + STEP[t]) % N, (rank - STEP[t]) % N
        lc, lp, ml = T["lc%d" % t], T["lp%d" % t], T["ml%d" % t]
        if t > 0:
            state(t)
        mm("pa", C, T.qp[:, 0:128], T.sp[:, 0:128], T.qt[:], T.st[:], ["qp0", "sp0", "qt"])
        mm("pb", C, T.qp[:, 128:256], T.sp[:, 128:256], T.qt[:], T.st[:], ["qp1", "sp1", "qt"])
        if t > 0:
            hoist("v", ["p8"], ["of", "oe", "se", "ses", "or", "ok", "tl", "fr", "ks", "d00", "d0h", "d01", "kk0", "kk1"]
                  + ["os%d" % m for m in range(4)] + fres + sres)
            hoist("a", (), ["sb0", "sb1", "d02", "d03", "rr", "cr"] + ["rk%d" % m for m in range(4)])
        halves = [slice(0, C // 2), slice(C // 2, C)]
        for h, s in enumerate(halves):
            ts(T.t1[:, s], T.pa[:, s], 0.0, 4.0, Alu.is_lt, Alu.mult, ["pspa"], ["k1%d" % h])
        spare("t1")
        for h, s in enumerate(halves):
            act(T.sb[:, s], T.pb[:, s], Act.Sign, ["pspb"], ["sb%d" % h], bias=2.0 ** -120)
            tt(T.t2[:, s], T.t1[:, s], T.p8[:, s], Alu.add, ["k1%d" % h, "p8"], ["k2%d" % h])
        spare("t2")
        for h, s in enumerate(halves):
            tt(T.kk[:, s], T.t2[:, s], T.sb[:, s], Alu.subtract, ["k2%d" % h, "sb%d" % h], ["kk%d" % h])
        kres = ["kk%d" % h for h in range(len(halves))]
        spare("kk")

        def dm(m):
            return T.d0[:, C * m:C * m + C]

        for m in range(4 - ACTD, 4):
            act(dm(m), T.kk[:, ::-1], Act.Abs, kres + ["kab"], ["d0%d" % m], scale=8.0 * FAR, bias=T.kab[:, m:m + 1])
        group(("d0", t), [ts(T.d0[:, C // 2:C], T.kk[:, C // 2 - 1::-1], T.kap[:, 0:1], FAR, Alu.not_equal, Alu.mult, ["kk0", "kap"], ["d0h"]),
                          ts(T.d0[:, 0:C // 2], T.kk[:, C - 1:C // 2 - 1:-1], T.kap[:, 0:1], FAR, Alu.not_equal, Alu.mult, ["kk1", "kap"], ["d00"])])
        for m in range(1, 4 - ACTD):
            ts(dm(m), T.kk[:, ::-1], T.kap[:, m:m + 1], FAR, Alu.not_equal, Alu.mult, kres + ["kap"], ["d0%d" % m])
        dres = [["d00", "d0h"], ["d01"], ["d02"], ["d03"]]
        spare("d0")
        group(("p1", t), [scan(T.p1[:, PS * m + 1:PS * m + 1 + C], dm(m), T.jr[:], pini[m], Alu.min, Alu.max,
                               dres[m] + ["jr", "ini"], [fres[m]]) for m in range(4)][1:])
        of = T.ms[:, M_F:M_F + 4]

        def next_member(m):
            group(("p2", t), [scan(T.p2[:, C * m:C * m + C], dm(m), T.p1[:, PS * m:PS * m + C], pini[m], Alu.min, Alu.max,
                                   dres[m] + [fres[m], "ini"], [sres[m]])])

        def count(m, row, res):
            return act(T.junk[:, K * m:K * m + K], row, Act.Sign, res + [fres[m]], ["rk%d" % m], scale=-0.5, bias=first[m],
                       accum_out=T.rk[:, m:m + 1])

        def halved(b):
            act(T.fh[:, PL * b:PL * b + C], T["f%d" % b][:, 0:C], Act.Copy, ["psf%d" % b], ["fh%d" % b], scale=0.5)

        def firsts(b):
            act(T.aa[:, K * b:K * b + K], T.fh[:, PL * b:PL * b + PL].indirect(ml[:, M_F:M_F + 4]), Act.Copy,
                ["fh%d" % b, "fz%d" % b, "lf%d" % t], ["fa%d" % b])

        def seconds(b):
            return tt(T.gg[:, K * slot[b]:K * slot[b] + K], T.fh[:, PL * b:PL * b + PL].indirect(ml[:, M_S:M_S + 4]),
                      T.aa[:, K * b:K * b + K], Alu.add, ["fh%d" % b, "fz%d" % b, "fa%d" % b, "ls%d" % t], ["gg%d" % b])

        def first_list():
            ts(of, T.p1[:, C:4 * PS:PS], 0.1, None, Alu.add, None, fres, ["of"])
            send(to, [(of, ml[:, M_F:M_F + 4])], "f%d" % t, ["of"])

        def ranks():
            cp(T.fr[:], T.iw[:].indirect(of), ["iw", "of"], ["fr"])
            group(("rk", t), [count(m, T.iw[:].indirect(of), ["iw", "of"]) for m in range(FUSED)]
                  + [count(m, T.fr[:], ["fr"]) for m in range(FUSED, 4)])
            for b in range(4 if t > 0 else 2):
                halved(b)

        arrival(frm, "t%d" % t, 2, ["lt%d" % t])
        for b in range(4):
            mm("f%d" % b, C, eq(b)[0], eq(b)[1], lc[:, 0:C], lp[:, 0:C], ["e%d" % b, "lt%d" % t])

        def second_list():
            group(("os", t), [ts(T.ms[:, M_S + m:M_S + m + 1], T.tl[:, m:m + 1], first[m], second[m], Alu.add, Alu.min,
                                 ["tl", fres[m], sres[m]], ["os%d" % m]) for m in range(4)])
            send(to, [(T.ms[:, M_S:M_S + 4], ml[:, M_S:M_S + 4])], "s%d" % t, ["os%d" % m for m in range(4)])

        steps = {
            "of": first_list, "fr": ranks, "os": second_list,
            "tl": lambda: ts(T.tl[:], T.p2[:, C - 1:4 * C:C], C - 0.5, FAR, Alu.is_lt, Alu.mult, sres, ["tl"]),
            "or": lambda: ts(off(O_R, 4), T.rk[:], 0.5, 32.1, Alu.mult, Alu.add, ["rk%d" % m for m in range(4)], ["or"]),
            "se": lambda: cp(T.se[:].indirect(off(O_R, 4)), T.i64[:], ["or", "i64"], ["se"]),
            "ses": lambda: scan(T.ses[:], T.cw8[:], T.se[:], 0.0, Alu.mult, Alu.add, ["cw8", "se"], ["ses"]),
            "ks": lambda: scan(T.ks[:], T.cw16[:], T.kk[:], 0.0, Alu.mult, Alu.add, ["cw16"] + kres, ["ks"]),
            "ok": lambda: ts(off(O_K, 12), T.ks[:, 15:C:16], col(C_M16K), 0.1, Alu.mult, Alu.add, ["ks", "cm16k"], ["ok"]),
        }
        for m in range(4):
            steps["n%d" % m] = lambda m=m: next_member(m)
        for name in ORDER.split():
            steps[name]()
            spare(name)
        ts(T.ms[:, M_E:M_E + 8], T.ses[:, 7:K:8], col(C_M8), col(C_A8), Alu.mult, Alu.add, ["ses", "cm8", "ca8"], ["oe"])
        send(to, [(T.ms[:, M_E:M_E + 8], ml[:, M_E:M_E + 8])], "e%d" % t, ["oe"])

        arrival(frm, "f%d" % t, 1, ["lf%d" % t])
        arrival(frm, "s%d" % t, 1, ["ls%d" % t])
        if t == 0:
            for step, b in ((firsts, 0), (halved, 2), (firsts, 1), (halved, 3), (firsts, 2), (firsts, 3)):
                step(b)
        else:
            for b in range(4):
                firsts(b)
        group(("gg", t), [seconds(b) for b in range(4)])
        act(T.rr[:], T.i64[:].indirect(off(O_R, 4)), Act.Copy, ["i64", "or"], ["rr"])
        gres = ["gg%d" % b for b in range(4)]

        def own_f():
            for b in range(4):
                mm("f%d" % b, C, eq(b)[0], eq(b)[1], T.qt[:], T.st[:], ["e%d" % b, "qt"])

        if t > 0:
            own_f()

        wb = ["pa", "pb", "x0", "x1"]
        hoist("v", gres, ["z1", "qz"])
        hoist("a", gres, ["z0"])
        hoist("p", ["qw", "sw"], ["ps" + b for b in wb])
        arrival(frm, "e%d" % t, 1, ["le%d" % t])
        group(("z", t), [
            act(T.zh[:, 0:256:2], T.gg[:, 0:128].indirect(ml[:, M_E:M_E + 8]), Act.Copy, gres + ["le%d" % t], ["z0"]),
            cp(T.zh[:, 1:256:2], T.gg[:, 128:256].indirect(ml[:, M_E:M_E + 8]), gres + ["le%d" % t], ["z1"])])
        quant(T.qz[:], T.sz[:], T.zh[:, 0:512], ["z0", "z1", "zero"], ["qz"])
        for b in range(4):
            mm(wb[b], 128, T.qw[:, 128 * b:128 * b + 128], T.sw[:, 128 * b:128 * b + 128], T.qz[:], T.sz[:], ["qw", "sw", "qz"])
        if t == 0:
            own_f()

        act(T.cr[:], T.rr[:].indirect(off(O_K, 12)), Act.Copy, ["rr", "ok"], ["cr"])
        scan(T.cs[:], T.cw16[:], T.cr[:], 0.0, Alu.mult, Alu.add, ["cw16", "cr"], ["cs"])
        ts(off(O_C, 12), T.cs[:, 15:C:16], col(C_M16), 0.1, Alu.mult, Alu.add, ["cs", "cm16"], ["oc"])
        hoist("v", (), ["qh", "h3"])
        hoist("a", (), ["h0", "h1", "h2"])
        ids = []
        for b in range(4):
            o, i = T.zh[:, 512 + b:768:4], T[wb[b]][:, 0:K]
            if b < 3:
                ids.append(act(o, i, Act.Relu, ["ps" + wb[b]], ["h%d" % b], scale=0.03125))
            else:
                ids.append(ts(o, i, 0.0, 0.03125, Alu.max, Alu.mult, ["ps" + wb[b]], ["h%d" % b]))
        group(("h", t), ids)
        quant(T.qh[:], T.sh[:], T.zh[:, 256:768], ["h0", "h1", "h2", "h3", "zero"], ["qh"])
        send(frm, [(u8(T.qh[:, K:2 * K]), u8(lc[:, C:C + K])), (T.sh[:, K:2 * K], lp[:, C:C + K])], "h%d" % t, ["qh"])

        if t < ROUNDS - 1:
            odd_row()
            own_row()
            pre_keys()
        else:
            ending.append(dma("s", T.ol[:], T.cr[0:128:16, :], ["cr"], ()))
            quant(T.qv[:], T.sv[:], T.vt[:], ["vt"], ["qv"])
        for b in range(3):
            act(T.fb[:, C * b:C * b + C], T["f%d" % b][:, 0:C], Act.Copy, ["psf%d" % b], ["ff%d" % b])

        db = ["x0", "x1", "pa", "pb"]
        hoist("v", (), ["qt", "dh0"] + tplanes)
        hoist("a", ["oc"], ["dh1", "dh2", "dh3", "tmp"])
        hoist("p", (), ["ps" + b for b in db])
        arrival(to, "h%d" % t, 2, ["lh%d" % t])
        if t == 0:
            dma("s", T.vt[:], T.v[:], ["lh0"], ["vt"])
        for b in (0, 1, 3, 2):
            mm(db[b], 128, eq(b)[0], eq(b)[1], lc[:, 128:256], lp[:, 128:256], ["e%d" % b, "lh%d" % t, "lt%d" % t])

        def dwin(b):
            return T.dh[:, K * b:K * b + K]

        def both(b):
            return tt(T.tt[:, b:4 * C:4], dwin(b).indirect(off(O_C, 12)), T.fb[:, C * b:C * b + C], Alu.add,
                      ["dh%d" % b, "oc", "ff%d" % b], [tplanes[b]])

        cp(dwin(0), T[db[0]][:, K:2 * K], ["ps" + db[0]], ["dh0"])
        hoist("v", ["ff0", "ff1", "ff2"])
        for b in (1, 3, 2):
            act(dwin(b), T[db[b]][:, K:2 * K], Act.Copy, ["ps" + db[b]], ["dh%d" % b])
        act(T.tmp[:], dwin(3).indirect(off(O_C, 12)), Act.Copy, ["dh3", "oc"], ["tmp"])
        group(("t", t), [both(0), both(1), both(2),
                         tt(T.tt[:, 3:4 * C:4], T.f3[:, 0:C], T.tmp[:], Alu.add, ["psf3", "tmp"], [tplanes[3]])])

    quant(T.qt[:], T.st[:], T.tt[:], tplanes, ["qt"])
    mm("x0", C, T.qv[:], T.sv[:], T.qt[:], T.st[:], ["qv", "qt"])
    ending.append(dma("s", T.oc[:], u8(T.qt[:]), ["qt"], ()))
    ids = [dma("s", T.osc[4 * k:4 * k + 4, :], T.st[32 * k:32 * k + 4, :], ["qt"], ()) for k in range(4)]
    group("osc", ids)
    ending.extend(ids)
    act(T.yo[:], T.x0[:, 0:C], Act.Copy, ["psx0"], ["yo"])
    ending.append(dma("a", T.y[:], T.yo[:], ["yo"], ()))
    op("g", None, (), (), after=ending)
    emit(g, T, ops)
